import numpy as np, ml_dtypes
CORES = [6,15,38,47]
N = 4
BF = ml_dtypes.bfloat16
def gentries(a):
    return np.ascontiguousarray(a.reshape(8, 16, -1).transpose(0, 2, 1)).reshape(8, -1)
def gtable(e):
    e = np.asarray(e); return np.ascontiguousarray(e.reshape(8, -1, 16).transpose(0, 2, 1)).reshape(128, -1).astype(np.int32)
C, NV, LN, RO, LV = 4096, 1024, 128, 3, 3
H, L, B, S = NV // 2, 2 * LN, C - LN * RO, LN // N
def parts(rng):
    o = np.argsort(rng.random((N, 8, C)), axis=-1); h = np.zeros((N, 8, C), np.int64)
    np.put_along_axis(h, o, np.broadcast_to(np.arange(C) * 256 // C, (N, 8, C)), 2)
    x = np.clip(h[:, :, None] + rng.integers(-60, 61, (N, 8, 16, C)), 0, 255)
    cen = rng.random((N, 8, NV, 1)); wd = rng.choice(np.array([0.02, 0.1, 0.3, 1.0]), (N, 8, NV, 1))
    pos = np.clip(((cen + wd * (rng.random((N, 8, NV, 16)) - 0.5)) * C).astype(np.int64), 0, C - 1)
    ring = np.take_along_axis(o, pos.reshape(N, 8, -1), 2).reshape(N, 8, NV, 16)
    ring = np.where(rng.random(ring.shape) < 0.04, C, ring)
    kid = rng.integers(0, NV, (N, 8, 2, NV)); rt = rng.integers(0, NV, (N, 8, L)); fn = rng.integers(0, C, (N, 8, LN))
    xl = np.clip(rng.integers(0, 256, (N, 8, 1, LN)) + rng.integers(-60, 61, (N, 8, 16, LN)), 0, 255)
    snd = np.argsort(rng.random((N, 8, LN)), axis=-1)
    return x, ring, kid, rt, xl, fn, snd
def plant(rng, ring, rt, fn):
    n, g, i = np.indices((N, 8, LN)); v = rt[..., LN:]; k = rng.integers(0, 16, (N, 8, LN))
    m = rng.random((N, 8, LN)) < 0.7; ring[n[m], g[m], v[m], k[m]] = fn[m]
    m = rng.random((N, 8, LN)) < 0.4; ring[n[m], g[m], v[m] ^ H, 15 - k[m]] = fn[m]
def pack(x, ring, kid, rt, xl, fn, snd):
    return {"x": np.ascontiguousarray(np.reshape(x, (N, 128, C))).astype(np.float32).astype(BF), "ring": np.ascontiguousarray(ring.transpose(0, 1, 3, 2)).reshape(N, 128, NV).astype(np.int32),
            "kid": np.ascontiguousarray(kid).reshape(N, 16, NV).astype(np.int32), "rt": np.stack([gtable(a) for a in rt]), "xl": np.reshape(xl, (N, 128, LN)).astype(np.float32).astype(BF),
            "fn": np.stack([gtable(a) for a in fn]), "snd": np.stack([gtable(a) for a in snd])}
def edge(rng, shape, top, share):
    r = rng.random(shape)
    return np.where(r < share * 0.5, 0, np.where(r < share, top, rng.integers(0, top + 1, shape)))
def halves(rng, *shape):
    k = shape[:-2] + (1, shape[-1])
    return 255 * np.where(rng.random(k) < 0.5, rng.integers(0, 2, k), rng.integers(0, 2, shape))
def swaps(rng, n, g, x, ring, rt, xl, fn, but):
    p = np.concatenate([np.array([0]), rng.permutation(np.arange(1, H - 1))[:L - 2], np.array([H - 1])])
    r = p + H * rng.integers(0, 2, L); r[0] = 0; r[L - 1] = NV - 1; rt[n, g] = r
    x[n, g, :, 0] = 255; x[n, g, :, C - 1] = 0
    hi = rng.integers(0, 2, L); xl[n, g] = 255 * hi[:LN]; fn[n, g] = np.where(hi[LN:] == 1, 0, C - 1)
    ring[n, g, r] = np.where(hi == 1, C, 0)[:, None]; ring[n, g, r ^ H] = np.where(hi == 1, 0, C)[:, None]
    if but: ring[n, g, r[L // 2] ^ H] = ring[n, g, r[L // 2]].copy()
def again(rng, n, g, x, ring, kid, rt, xl, fn, snd):
    o = rng.permutation(H); r = o[:L] + H * rng.integers(0, 2, L); rt[n, g] = r; i = np.arange(LN); h = LN // 2
    gap = np.array([2, L - 2, L, L, L + 2, 2 * L])
    x[n, g, :, 0] = 255; x[n, g, :, 1:7] = (2040 + gap[None, :] // 2 + np.arange(16)[:, None]) // 16
    xl[n, g] = 255; fn[n, g] = np.where(i < h, 0, 1 + i % 6); snd[n, g, :S] = h + np.arange(S)
    good = np.concatenate([np.zeros(LN, np.int64), fn[n, g]])[:, None]
    ring[n, g, r] = C; ring[n, g, r ^ H] = good
    if LV == 2: kid[n, g][:, r] = r ^ H
    else:
        q = o[L:2 * L] + H * rng.integers(0, 2, L); ring[n, g, q] = C; ring[n, g, q ^ H] = good
        kid[n, g][:, r] = q; kid[n, g][:, q] = r ^ H
def setup_inputs(rng):
    x, ring, kid, rt, xl, fn, snd = parts(rng); plant(rng, ring, rt, fn)
    return pack(x, ring, kid, rt, xl, fn, snd)
def setup_inputs_spread(rng):
    x, ring, kid, rt, xl, fn, snd = parts(rng)
    x = np.minimum(np.exp2(8 * rng.random((N, 8, 1, C))) * rng.random((N, 8, 16, C)), 255).astype(np.int64)
    xl = np.minimum(np.exp2(8 * rng.random((N, 8, 1, LN))) * rng.random((N, 8, 16, LN)), 255).astype(np.int64)
    ring = rng.integers(0, C + 1, ring.shape); plant(rng, ring, rt, fn)
    return pack(x, ring, kid, rt, xl, fn, snd)
def setup_inputs_ends(rng):
    x, ring, kid, rt, xl, fn, snd = parts(rng)
    x = halves(rng, N, 8, 16, C); xl = halves(rng, N, 8, 16, LN); x[:, ::2, :, 0] = 255
    ring = edge(rng, ring.shape, C, 0.64); ring[:, :, 5::16, :15] = C; ring[:, :, 5::16, 15] = 0; ring[:, :, 10::16, :15] = 0; ring[:, :, 10::16, 15] = C
    kid = edge(rng, kid.shape, NV - 1, 0.66); rt = edge(rng, rt.shape, NV - 1, 0.9); snd = edge(rng, snd.shape, LN - 1, 0.7)
    fn = (C - 1) * rng.integers(0, 2, fn.shape)
    for n in range(N):
        for g in (3, 7): swaps(rng, n, g, x, ring, rt, xl, fn, False)
    return pack(x, ring, kid, rt, xl, fn, snd)
def setup_inputs_corners(rng):
    x, ring, kid, rt, xl, fn, snd = parts(rng); plant(rng, ring, rt, fn); node = np.arange(NV)
    for n in range(N):
        s = int(rng.integers(0, 8))
        for g in range(8):
            m = (g + s) % 8
            if m == 0: ring[n, g] = C
            if m == 1: ring[n, g] = ring[n, g, :, :1].copy(); ring[n, g, rt[n, g, LN:]] = fn[n, g][:, None]
            if m == 2: kid[n, g] = node; rt[n, g] = rng.permutation(H)[:L] + H * rng.integers(0, 2, L); ring[n, g, rt[n, g]] = rng.permutation(C)[:L, None]
            if m == 3: kid[n, g] = node ^ H
            if m == 4: kid[n, g, 0] = (node + 1) % NV; kid[n, g, 1] = NV - 1; rt[n, g, ::4] = NV - 1; rt[n, g, 1::4] = 0
            if m == 5: ring[n, g] = rng.integers(B, C, (NV, 16)); fn[n, g] = rng.integers(B, B + LN, LN)
            if m == 6: rt[n, g] = rng.choice(np.array([0, H - 1, H, NV - 1]), L); kid[n, g] = (NV - 1) * rng.integers(0, 2, (2, NV))
            if m == 7: snd[n, g] = (LN - 1) * (n % 2); fn[n, g] = rng.integers(0, C)
    return pack(x, ring, kid, rt, xl, fn, snd)
def setup_inputs_crowd(rng):
    x, ring, kid, rt, xl, fn, snd = parts(rng); plant(rng, ring, rt, fn)
    for n in range(N):
        s = int(rng.integers(0, 8))
        for g in range(8):
            m = (g + s) % 8; v = int(rng.integers(0, NV)); c = int(rng.integers(0, C))
            if m == 0: again(rng, n, g, x, ring, kid, rt, xl, fn, snd)
            if m == 1: swaps(rng, n, g, x, ring, rt, xl, fn, True)
            if m == 2: rt[n, g] = v
            if m == 3: rt[n, g] = v; rt[n, g, L - 1] = (v + 1) % NV
            if m == 4: rt[n, g] = v ^ (H * rng.integers(0, 2, L))
            if m == 5: ring[n, g] = c
            if m == 6: ring[n, g] = c; rt[n, g, 0] = v; ring[n, g, v] = (c + 1) % C; rt[n, g, 1:] = np.where(rt[n, g, 1:] == v, (v + 1) % NV, rt[n, g, 1:])
            if m == 7: rt[n, g] = v; kid[n, g] = rng.integers(0, NV); fn[n, g] = c; ring[n, g, v, ::2] = c; snd[n, g] = rng.integers(0, LN)
    return pack(x, ring, kid, rt, xl, fn, snd)
def setup_inputs_ties(rng):
    x, ring, kid, rt, xl, fn, snd = parts(rng)
    b = rng.choice(np.array([0, 100, 252]), (N, 8, 1, 1)); s = rng.choice(np.array([1, 2, 3]), (N, 8, 1, 1))
    x = b + s * rng.integers(0, 2, x.shape); xl = b + s * rng.integers(0, 2, xl.shape)
    q = rng.choice(np.array([1, 2, 3, 16]), (N, 8, NV, 1)); ring = np.take_along_axis(ring, rng.integers(0, 16, ring.shape) % q, 3)
    pool = rng.integers(0, NV, (N, 4, 12)); rt[:, ::2] = np.take_along_axis(pool, rng.integers(0, 12, (N, 4, L)), 2)
    plant(rng, ring, rt, fn)
    return pack(x, ring, kid, rt, xl, fn, snd)
def check_inputs(d):
    bad = []
    for k, lo, hi in (("x", 0, 255), ("ring", 0, C), ("kid", 0, NV - 1), ("rt", 0, NV - 1), ("xl", 0, 255), ("fn", 0, C - 1), ("snd", 0, LN - 1)):
        a = np.asarray(d[k]).astype(np.float64)
        if not (np.min(a) >= lo and np.max(a) <= hi): bad.append("range of " + k)
        elif np.any(a != np.floor(a)): bad.append("whole numbers in " + k)
    return bad
def first(key, on):
    low = np.arange(L)[:, None] > np.arange(L)[None, :]
    return on & ~np.any((key[..., :, None] == key[..., None, :]) & on[..., None, :] & low, axis=-1)
def reference(x, ring, kid, rt, xl, fn, snd):
    X = np.zeros((N, 8, 16, C + 1), np.int32); X[..., :C] = x.astype(np.float32).astype(np.int32).reshape(N, 8, 16, C)
    R = ring.astype(np.int32).reshape(N, 8, 16, NV); K = kid.astype(np.int32).reshape(N, 8, 2, NV)
    st = np.stack([gentries(a) for a in rt]).astype(np.int64).reshape(N, 8, 2, LN); to = np.stack([gentries(a) for a in snd]).astype(np.int64)
    fname = np.stack([gentries(a) for a in fn]).astype(np.int64); come = xl.astype(np.float32).astype(np.int32).reshape(N, 8, 16, LN)
    A = np.zeros((N, 8, 1), np.int64)
    for t in range(RO):
        p0 = B + LN * t; X[..., p0:p0 + LN] = come
        lname = np.broadcast_to(p0 + np.arange(LN), (N, 8, LN)); name = np.concatenate([lname, fname], axis=2)
        w = np.take_along_axis(X, name[:, :, None, :], 3)
        v = np.concatenate([st[:, :, t & 1], st[:, :, (t + 1) & 1]], axis=2); new = np.zeros((N, 8, NV), bool)
        for l in range(LV):
            u = v ^ H
            rv = np.take_along_axis(R, v[:, :, None, :], 3); ru = np.take_along_axis(R, u[:, :, None, :], 3)
            z = np.take_along_axis(X, rv.reshape(N, 8, 1, 16 * L), 3).reshape(N, 8, 16, 16, L)
            zu = np.take_along_axis(X, ru.reshape(N, 8, 1, 16 * L), 3).reshape(N, 8, 16, 16, L)
            m = (np.max(z, axis=3) + np.min(z, axis=3)) >> 1; mu = (np.max(zu, axis=3) + np.min(zu, axis=3)) >> 1
            near = np.argmin(np.add.reduce(np.abs(z - w[:, :, :, None, :]), axis=2), axis=2)
            c = np.take_along_axis(rv, near[:, :, None, :], 2)[:, :, 0]
            dv = np.add.reduce(np.abs(w - m), axis=2); du = np.add.reduce(np.abs(w - mu), axis=2)
            b = np.count_nonzero(w >= m, axis=2) >= 9
            act = first(v & (H - 1), np.ones((N, 8, L), bool)); ex = act & (du + A < dv)
            kv = np.take_along_axis(K, v[:, :, None, :], 3); nxt = np.where(b, kv[:, :, 1], kv[:, :, 0]).astype(np.int64)
            n, g, j = np.nonzero(first(c, c < C)); a = c[n, g, j]
            X[n, g, :, a] = (X[n, g, :, a] + w[n, g, :, j]) >> 1
            n, g, j = np.nonzero(ex); a = v[n, g, j]; e = u[n, g, j]
            R[n, g, :, a] = ru[n, g, :, j]; R[n, g, :, e] = rv[n, g, :, j]
            ka = K[n, g, :, a].copy(); ke = K[n, g, :, e].copy(); K[n, g, :, a] = ke; K[n, g, :, e] = ka
            new[n, g, a] = True; new[n, g, e] = True
            n, g, j = np.nonzero(act[..., :LN]); R[n, g, (j + t) & 15, v[n, g, j]] = p0 + j
            n, g, j = np.nonzero(act[..., LN:]); j = j + LN; a = v[n, g, j]; col = R[n, g, :, a]
            R[n, g, :, a] = np.where((col == name[n, g, j][:, None]) & ~new[n, g, a][:, None], C, col)
            A = np.count_nonzero(ex, axis=2)[..., None]
            if l < LV - 1: v = nxt
        if t < RO - 1:
            gone = np.take_along_axis(X, fname[:, :, None, :], 3); come = np.zeros((N, 8, 16, LN), np.int32)
            for q in range(N):
                for d in range(N): come[(q + d) % N, :, :, d * S:d * S + S] = np.take_along_axis(gone[q], to[q][:, None, d * S:d * S + S], 2)
            fname = lname
    return {"yx": X[..., :C].astype(np.float32).astype(BF).reshape(N, 128, C), "yr": R.reshape(N, 128, NV).astype(np.float32), "yk": K.reshape(N, 16, NV).astype(np.float32)}

@@ -1,0 +1,629 @@
+from concourse.bass import DstId, RemoteDMATransfer
+from concourse.mybir import AluOpType as O, ActivationFunctionType as F, AxisListType
+
+BF, FP, I32, U16 = "bfloat16", "float32", "int32", "uint16"
+XW = 4096 + 16 + 256
+XD = 4096 + 16
+RW = 1024 + 768
+SW = 512 + 256
+MAGIC = 12582912.0
+NV = 3
+NU = 0
+CYC, PCYC, GAM, SIG, WAKE = 0.83e-3, 0.83e-3, 1.5, 3.0, 0.08
+
+
+def _s(cols, dt):
+    return ("sbuf", [128] + (cols if isinstance(cols, list) else [cols]), dt)
+
+
+SCRATCH = {
+    "X": _s(XW, BF), "RT": _s(RW, FP), "RI": _s(1024, I32), "IDX": _s(4112, FP), "KT": _s(1024, BF), "ST": _s(SW, FP),
+    "ZV": _s(4096, BF), "ZU": _s(4096, BF), "DAB": _s([16, 256], BF), "MXV": _s(4096, BF), "MNV": _s(4096, BF),
+    "MXU": _s(4096, BF), "MNU": _s(4096, BF), "YK": _s(1024, BF), "WREP": _s(4096, BF), "W": _s(256, BF),
+    "MKX": _s(1024, BF), "MKN": _s(1024, BF), "RSK": _s(256, FP), "SLOT": _s(256, BF), "THR": _s(256, BF),
+    "CQ": _s(256, BF), "HALF": _s(16, BF), "ROWS": _s(128, BF), "ROWT": _s(128, BF), "ROW1": _s(128, BF),
+    "SELB": _s(2048, BF), "SEL32": _s(2048, BF), "SELK0": _s(2048, BF), "SELDK": _s(2048, BF),
+    "ID": _s(128, BF), "IDH": _s(128, BF), "IDN": _s(128, BF), "BLK": _s(128, BF), "WD": _s(128, BF), "WO": _s(128, BF),
+    "SWP": _s(512, FP), "MFH": _s([2, 4, 32], FP), "SELY": _s(16, BF),
+    "PC": _s(1, I32), "PA": _s(8, I32), "PF": _s(16, FP), "MI": _s(128, I32), "MJ": _s(128, I32), "MF": _s(512, FP),
+    "LQ": _s(128, I32), "LF": _s(128, FP), "NR0": _s(128, FP), "NR1": _s(128, FP), "NR2": _s(128, FP),
+    "LO0": _s(768, FP), "LO1": _s(768, FP), "LO2": _s(768, FP), "HI0": _s(128, FP), "HI1": _s(128, FP), "HI2": _s(128, FP),
+    "D64": _s(64, FP), "DX": _s(16, FP), "KI": _s(1024, I32), "KH": _s(1024, FP), "KL": _s(1024, FP),
+    "RTI": _s(16, I32), "RTF": _s(16, FP), "RTS": _s(16, FP), "FNI": _s(8, I32), "SNI": _s(8, I32), "F16": _s(8, U16), "S16": _s(8, U16),
+    "NMF": _s(128, FP), "GI": _s(128, I32), "GH": _s(256, BF),
+    "HN0": _s(8, U16), "HN1": _s(8, U16), "N16": _s(16, U16), "HB0": _s(128, BF), "HB1": _s(128, BF), "CM0": _s(128, BF), "CM1": _s(128, BF),
+    "VB": _s(64, FP), "V16": _s(32, U16), "P16": _s(32, U16), "T1": _s(64, FP), "T2": _s(64, FP), "UM": _s(32, FP),
+    "RV16": _s(256, U16), "RU16": _s(256, U16), "VAL": _s(768, FP), "TV": _s([8, 32], FP),
+    "KRP": _s(256, U16), "KRC": _s(256, U16), "EP": _s([16, 272], BF), "EC": _s([16, 272], BF), "SG": _s(256, BF),
+    "AA": _s(64, FP), "AC0": _s(16, FP), "AC1": _s(16, FP), "MR": _s(256, BF), "MS": _s(256, FP), "ML": _s(32, FP), "FRW": _s(256, BF),
+    "HR": _s(512, FP), "QV": _s(512, BF), "QU": _s(256, BF), "GV": _s(16, FP), "BF1": _s(32, FP), "TD": _s(64, FP), "C64": _s(64, FP), "OFF": _s(64, U16),
+    "EXB": _s(16, BF), "AX": _s(2, FP), "FK": _s(256, FP), "UE": _s(256, FP), "UN": _s(256, FP), "NU": _s(256, FP), "CN": _s(256, FP),
+    "CL": _s(64, FP), "C16": _s(32, U16), "XC": _s(256, BF), "RD": _s(256, FP), "DR": _s(256, BF),
+    "P0": ("psum", [128, 512], FP), "PR": ("psum", [128, 8, 64], FP), "P1": ("psum", [128, 512], FP), "P2": ("psum", [128, 512], FP),
+    "P3": ("psum", [128, 512], FP), "P4": ("psum", [128, 512], FP), "P6": ("psum", [128, 512], FP), "P7": ("psum", [128, 512], FP),
+}
+QS = ["qV", "qS", "qP", "qG"]
+SEMAPHORES = QS + ["d%d" % i for i in range(16)] + ["arr0", "arr1", "out0", "out1"]
+ISZ = {BF: 2, U16: 2, FP: 4, I32: 4}
+
+
+def _psum(n):
+    return SCRATCH[n][0] == "psum"
+
+
+def _plan(nodes):
+    N = len(nodes)
+    succ = [[] for _ in range(N)]
+    npre = [0] * N
+    recs, lastp = {}, {}
+    for i, (eng, call, reads, writes, cost, lat, kind) in enumerate(nodes):
+        pre = {}
+        for (n, lo, hi) in reads:
+            for r in recs.get(n, []):
+                if (_psum(n) and r[4] != eng) or (r[2] and r[0] < hi and lo < r[1]):
+                    pre[r[3]] = WAKE
+        for (n, lo, hi) in writes:
+            ps = _psum(n)
+            if ps and eng == "qP" and n in lastp:
+                pre.setdefault(lastp[n], 0.0)
+            for r in recs.get(n, []):
+                if (ps and r[4] != eng) or (r[0] < hi and lo < r[1] and not (ps and eng == "qP")):
+                    pre[r[3]] = WAKE
+            if ps and eng == "qP":
+                lastp[n] = i
+        for j, w in pre.items():
+            succ[j].append((i, w))
+        npre[i] = len(pre)
+        for (n, lo, hi) in writes:
+            recs[n] = [r for r in recs.get(n, []) if not (lo <= r[0] and r[1] <= hi)]
+        for (n, lo, hi) in writes:
+            recs[n].append((lo, hi, True, i, eng))
+        for (n, lo, hi) in reads:
+            recs.setdefault(n, []).append((lo, hi, False, i, eng))
+    prio = [0.0] * N
+    for i in range(N - 1, -1, -1):
+        b = 0.0
+        for j, w in succ[i]:
+            b = max(b, prio[j] + w)
+        prio[i] = b + nodes[i][5]
+    ready = {}
+    rt = [0.0] * N
+    for i in range(N):
+        if npre[i] == 0:
+            ready.setdefault(nodes[i][0], []).append(i)
+    free = {}
+    order = []
+    for _ in range(N):
+        best, bs = None, 0.0
+        for q, l in ready.items():
+            if l:
+                s = max(free.get(q, 0.0), min(rt[i] for i in l))
+                if best is None or s < bs:
+                    best, bs = q, s
+        l = ready[best]
+        k = max((i for i in l if rt[i] <= bs), key=lambda i: (prio[i], -i))
+        l.remove(k)
+        order.append(k)
+        free[best] = bs + nodes[k][4]
+        for j, w in succ[k]:
+            rt[j] = max(rt[j], bs + nodes[k][5] + w)
+            npre[j] -= 1
+            if npre[j] == 0:
+                ready.setdefault(nodes[j][0], []).append(j)
+    return order
+
+
+def rank_program(g, core, T, topo):
+    rank = T.rank_of(core)
+    if rank is None:
+        return
+    Q = {"qV": g.vector, "qS": g.scalar, "qP": g.tensor, "qG": g, "qY": g.sync}
+    nodes = []
+
+    def B(n, lo=0, hi=None, st=1):
+        t = T[n]
+        hi = SCRATCH[n][1][1] if hi is None else hi
+        ap = t[:, lo:hi] if st == 1 else t[:, lo:hi:st]
+        return (ap, [(n, lo, hi)], [], (hi - lo + st - 1) // st, ISZ[SCRATCH[n][2]], "p" if _psum(n) else "s")
+
+    def M(n, ap, lo, hi, k):
+        return (ap, [(n, lo, hi)], [], k, ISZ[SCRATCH[n][2]], "p" if _psum(n) else "s")
+
+    def IN(win, off, lo, hi):
+        return (T[win][:].indirect(T[off][:, lo:hi]), [(win, 0, 1 << 20), (off, lo, hi)], [], 16 * (hi - lo), 2, "i")
+
+    def OUT(win, off, lo, hi):
+        return (T[win][:].indirect(T[off][:, lo:hi]), [(win, 0, 1 << 20)], [(off, lo, hi)], 16 * (hi - lo), 2, "i")
+
+    def a(o):
+        return o[0]
+
+    def add(eng, outs, ins, cost, call, lat=None, kind="c"):
+        reads = [x for o in ins for x in o[1]] + [x for o in outs for x in o[2]]
+        writes = [x for o in outs for x in o[1]]
+        nodes.append((eng, call, reads, writes, cost, cost if lat is None else lat, kind))
+
+    def vc(out, ins, two=False):
+        if any(x[5] == "i" for x in ins):
+            return 0.05 + max(x[3] for x in ins) * GAM * CYC
+        if out[5] == "i":
+            return 0.05 + out[3] * SIG * CYC
+        n = out[3]
+        c = 0.5 * n if all(x[4] == 2 for x in ins + [out]) and not two else n
+        if two and all(x[5] == "s" for x in ins):
+            c = 2 * n
+        return max(64, c) * CYC
+
+    def tt(out, x, y, op):
+        add("qV", [out], [x, y], vc(out, [x, y], True), lambda: g.vector.tensor_tensor(a(out), a(x), a(y), op))
+
+    def ts(out, x, s1, s2, op0, op1=None):
+        cs = [s for s in (s1, s2) if isinstance(s, tuple)]
+        p1 = s1[0] if isinstance(s1, tuple) else s1
+        p2 = s2[0] if isinstance(s2, tuple) else s2
+        if op1 is None:
+            add("qV", [out], [x] + cs, vc(out, [x]), lambda: g.vector.tensor_scalar(a(out), a(x), p1, None, op0))
+        else:
+            add("qV", [out], [x] + cs, vc(out, [x]), lambda: g.vector.tensor_scalar(a(out), a(x), p1, p2, op0, op1))
+
+    def cp(out, x):
+        add("qV", [out], [x], vc(out, [x]), lambda: g.vector.tensor_copy(a(out), a(x)))
+
+    def ms(out, c):
+        add("qV", [out], [], vc(out, []), lambda: g.vector.memset(a(out), c))
+
+    def scan(out, d0, d1, init, op0, op1):
+        add("qV", [out], [d0, d1], vc(out, [d0, d1]), lambda: g.vector.tensor_tensor_scan(a(out), a(d0), a(d1), init, op0, op1))
+
+    def tr(out, x):
+        add("qV", [out], [x], vc(out, [x]), lambda: g.vector.transpose(a(out), a(x)))
+
+    def act(out, x, f, bias=0.0, scale=1.0):
+        cs = [s for s in (bias, scale) if isinstance(s, tuple)]
+        pb = bias[0] if isinstance(bias, tuple) else bias
+        sc = scale[0] if isinstance(scale, tuple) else scale
+        c = 0.065 + x[3] * GAM * CYC if x[5] == "i" else max(64, out[3]) * CYC
+        add("qS", [out], [x] + cs, c, lambda: g.scalar.activation(a(out), a(x), f, bias=pb, scale=sc))
+
+    def mm(out, l, r, start, stop):
+        c = max(min(64, l[3]), r[3]) * PCYC * (4 if l[4] == 4 else 1)
+        add("qP", [out], [l, r], c, lambda: g.tensor.matmul(a(out), a(l), a(r), start, stop))
+
+    def iota(out, pattern, base, cm):
+        add("qG", [out], [], 0.13 + 2 * out[3] * CYC,
+            lambda: g.iota(a(out), pattern, base, cm, allow_small_or_imprecise_dtypes=True))
+
+    def dma(eng, out, in_, kb):
+        add(eng, [out], [in_], 0.06, lambda: Q[eng].dma_start(a(out), a(in_)), 2.0 + kb / 250.0, "d")
+
+    def ext(ap):
+        return (ap, [], [], 0, 4, "d")
+
+    def sel(n, p):
+        return B(n, 128 * p, 128 * p + 128)
+
+    def tolist(ps, lo, S, row, rlo, rhi, start=True):
+        w = (rhi - rlo) // 16
+        for p in range(16):
+            mm(B(ps, lo, lo + w), sel(S, p), B(row, rlo + p, rhi, 16), start and p == 0, p == 15)
+
+    dma("qY", B("RTI"), ext(T.rt[:]), 8)
+    dma("qS", B("RI"), ext(T.ring[:]), 512)
+    dma("qY", B("X", 0, 1856), ext(T.x[:, 0:1856]), 464)
+    dma("qS", B("X", 1856, 3712), ext(T.x[:, 1856:3712]), 464)
+    dma("qY", B("X", 3840, 4096), ext(T.x[:, 3840:4096]), 64)
+    dma("qS", B("X", 3712, 3840), ext(T.xl[:]), 32)
+    dma("qY", B("FNI"), ext(T.fn[:]), 4)
+    dma("qY", B("SNI"), ext(T.snd[:]), 4)
+
+    iota(B("PC"), [[0, 1]], 0, 1)
+    iota(B("MI"), [[1, 128]], 0, 0)
+    iota(B("MF", 0, 64), [[16, 64]], 0, 0)
+    iota(B("LF"), [[1, 128]], 0, 0)
+    iota(B("IDX", 0, 1024), [[1, 1024]], 0, 0)
+    iota(B("IDX", 1024, 4112), [[1, 3088]], 1024, 0)
+    iota(B("KI"), [[0, 1024]], 0, 0)
+    for r in range(4):
+        k = r // 2
+        dma("qY", M("KI", T.KI[r:128:16, :], 0, 1024, 1024), ext(T.kid[k:16:2, :]), 64)
+
+    pf = lambda i: B("PF", i, i + 1)
+    ts(B("PA", 0, 1), B("PC"), 4, None, O.arith_shift_right)
+    ts(B("PA", 1, 2), B("PC"), 15, None, O.bitwise_and)
+    cp(B("PF", 0, 1), B("PC"))
+    cp(B("PF", 1, 3), B("PA", 0, 2))
+    ts(B("MJ"), B("MI"), 4, None, O.arith_shift_right)
+    cp(B("MF", 64, 192), B("MI"))
+    cp(B("MF", 192, 320), B("MJ"))
+    ts(B("ID"), B("MF", 64, 192), pf(0), None, O.is_equal)
+    act(B("IDH"), B("ID"), F.Copy, scale=0.5)
+    act(B("IDN"), B("ID"), F.Copy, scale=-1.0)
+    ts(B("BLK"), B("MF", 192, 320), pf(1), None, O.is_equal)
+    act(B("WO"), B("BLK"), F.Copy, scale=65536.0)
+    ms(B("SELB"), 0.0)
+    for p in range(16):
+        cp(B("SELB", 129 * p, 128 * p + 128, 16), B("BLK", 0, 128, 16))
+    act(B("SEL32"), B("SELB"), F.Copy, scale=1.0 / 32)
+    for i in range(4):
+        ts(B("PA", 2 + i, 3 + i), B("PA", 1, 2), i, 1, O.arith_shift_right, O.bitwise_and)
+    for i in range(4):
+        ts(pf(10 + i), B("PA", 2 + i, 3 + i), 2.0 ** -(1 << i) - 1.0, 1.0, O.mult, O.add)
+    tt(pf(14), pf(10), pf(11), O.mult)
+    tt(pf(15), pf(12), pf(13), O.mult)
+    tt(pf(14), pf(14), pf(15), O.mult)
+    ts(pf(3), pf(14), 32768.0, None, O.mult)
+    ts(B("WD"), B("BLK"), pf(3), None, O.mult)
+    ts(pf(7), pf(0), 0.0, None, O.is_equal)
+    ts(B("ROW1"), B("BLK"), 0.0, pf(7), O.mult, O.add)
+    ts(B("ROWS"), B("ROW1"), 1.0 / 16, None, O.mult)
+    iota(B("SLOT"), [[0, 16], [1, 16]], 0, 0)
+    ms(B("HALF"), 0.5)
+    ms(B("CQ"), -0.25)
+    ts(pf(15), pf(0), 16.0, -2.5, O.is_lt, O.mult)
+    tt(pf(15), pf(15), pf(3), O.mult)
+    ts(B("ROWT"), B("BLK"), 0.0, pf(15), O.mult, O.add)
+    iota(B("FK"), [[0, 16], [1, 16]], 0, 0)
+    ts(B("THR"), B("FK"), pf(2), None, O.is_equal)
+    cp(B("RT", 0, 1024), B("RI"))
+    cp(B("RTF"), B("RTI"))
+    cp(B("RTS", 0, 8), B("RTI", 8, 16))
+    cp(B("RTS", 8, 16), B("RTI", 0, 8))
+    ts(B("D64", 0, 48), B("MF", 0, 48), 1024.0, pf(2), O.add, O.add)
+    ts(B("D64", 48, 64), B("MF", 0, 16), 512.0, pf(2), O.add, O.add)
+    ts(B("DX"), B("MF", 0, 16), float(XD), pf(2), O.add, O.add)
+    ms(B("X", 4096, XW), 0.0)
+    iota(B("ST"), [[0, SW]], 1, 0)
+    ms(B("MKX"), 512.0)
+    ms(B("MKX", 0, 1024, 16), -512.0)
+    iota(B("MKN"), [[0, 1024]], -512, 0)
+    ms(B("MKN", 0, 1024, 16), 512.0)
+    ms(B("AX"), 0.0)
+
+    def nodelists():
+        ts(B("UM", 0, 16), B("VB", 0, 16), 512.0, 0.5, O.is_lt, O.subtract)
+        ts(B("UM", 16, 32), B("UM", 0, 16), 1024.0, None, O.mult)
+        tt(B("VB", 32, 48), B("VB", 0, 16), B("UM", 16, 32), O.add)
+        cp(B("V16", 16, 32), B("VB", 32, 48))
+
+    def pairs():
+        tt(B("T1", 0, 16), B("VB", 0, 16), B("VB", 32, 48), O.add)
+        ts(B("VB", 48, 64), B("T1", 0, 16), 0.5, -256.0, O.mult, O.add)
+        cp(B("P16", 0, 16), B("VB", 48, 64))
+
+    def compare(key, klo, k16, KR, E):
+        if KR == "KRP":
+            act(B("UN"), IN("IDX", k16, 0, 16), F.Copy)
+            cp(B(KR), B("UN"))
+        else:
+            cp(B(KR), IN("IDX", k16, 0, 16))
+        for q in range(16):
+            n = 256 - 16 * q
+            ts(M(E, T[E][:, q, 0:n], 272 * q, 272 * q + n, n), B(KR, 16 * q, 256), B(key, klo + q, klo + q + 1), None, O.is_equal)
+        mm(B("P2", 0, 256), B("ROWT"), B("THR"), True, False)
+        for q in range(15):
+            n = 256 - 16 * q
+            mm(B("P2", 16 * q + 16, 256), B("WO"), M(E, T[E][:, q, 16:n], 272 * q + 16, 272 * q + n, n - 16), False, False)
+        mm(B("P2", 0, 256), B("WD"), M(E, T[E][:, :, 0:16], 0, 16 * 272, 256), False, True)
+
+    def firsts(lo):
+        act(B("SG"), B("P2", 0, 256), F.Sign, scale=-1.0)
+        mm(B("P2", lo, lo + 16), B("ROW1"), B("HALF"), True, False)
+        tolist("P2", lo, "SEL32", "SG", 0, 256, False)
+
+    for t in (0, 1):
+        cp(B("VB", 0, 16), B("RTS" if t else "RTF"))
+        nodelists()
+        pairs()
+        compare("VB", 48, "P16", "KRP", "EP")
+        firsts(272)
+        cp(B("AC%d" % t), B("P2", 272, 288))
+
+    cp(B("F16"), B("FNI"))
+    cp(B("S16"), B("SNI"))
+    cp(B("NR0"), IN("IDX", "F16", 0, 8))
+    ts(B("NR1"), B("LF"), 3712.0, None, O.add)
+    ts(B("NR2"), B("LF"), 3840.0, None, O.add)
+    act(B("NMF"), IN("NR0", "S16", 0, 8), F.Copy)
+    cp(B("GI"), B("NMF"))
+    ts(B("LQ"), B("GI"), 63, None, O.bitwise_and)
+    ts(B("GI"), B("GI"), 6, None, O.arith_shift_right)
+    ts(B("GH", 0, 128), B("GI"), 4.0, None, O.mult)
+    ts(B("GH", 128, 256), B("LQ"), 1.0 / 16, None, O.mult)
+    for h in range(2):
+        for p in range(16):
+            mm(B("P4", 64, 72), sel("SELB", p), B("GH", 128 * h + p, 128 * h + 128, 16), h + p == 0, h * p == 15)
+    cp(B("HN0"), B("P4", 64, 72))
+    ts(B("HN1"), B("SNI"), 3712.0, None, O.add)
+    for t in range(3):
+        ts(B("GI"), B("MI"), float(t), None, O.add)
+        ts(B("LQ"), B("GI"), 15, None, O.bitwise_and)
+        ts(B("LF"), B("LQ"), pf(2), None, O.is_equal)
+        ts(B("MF", 384, 512), B("MF", 64, 192), 3712.0 + 128 * t, None, O.add)
+        L = "LO%d" % t
+        iota(B(L, 384, 768), [[0, 384]], 0, 0)
+        tt(B(L, 0, 128), B("LF"), B("MF", 384, 512), O.mult)
+        act(B(L, 256, 384), B(L, 0, 128), F.Copy)
+        ts(B("NMF"), B("MF", 384, 512), -5000.0, None, O.add)
+        tt(B("NMF"), B("NMF"), B("LF"), O.mult)
+        act(B("HI%d" % t), B("NMF"), F.Copy, bias=5000.0)
+    ms(B("RSK"), -1.0)
+    ms(B("RSK", 0, 256, 16), 100000.0)
+    iota(B("MFH"), [[0, 2], [32, 4], [0, 32]], -1000, 0)
+    for h in range(2):
+        iota(M("MFH", T.MFH[:, h, :, 16 * h:16 * h + 16], 0, 2, 64), [[32, 4], [1, 16]], 16 * h, 0)
+    for e in range(2):
+        for h in range(2):
+            i = 2 * e + h
+            ts(B("T1", i, i + 1), pf(0), -16.0 * (e - h), None, O.add)
+            ts(B("SWP", 128 * i, 128 * i + 128), M("MFH", T.MFH[:, h, :, :], 0, 2, 128), B("T1", i, i + 1), None, O.is_equal)
+    for (c, p, v) in ((4, 0, 32.0), (10, 1, 1.0), (5, 2, 32.0), (11, 3, 1.0)):
+        ts(pf(c), pf(2), float(p), v, O.is_equal, O.mult)
+    tt(pf(9), pf(10), pf(11), O.add)
+    tt(pf(8), pf(4), pf(5), O.add)
+    ts(pf(8), pf(8), 1.0 / 32, None, O.mult)
+    ts(pf(9), pf(9), 32.0, None, O.mult)
+    tt(pf(8), pf(8), pf(9), O.add)
+    tt(pf(4), pf(4), pf(10), O.add)
+    tt(pf(5), pf(5), pf(11), O.add)
+    tt(pf(6), pf(5), pf(4), O.subtract)
+    act(B("SELK0"), B("SELB"), F.Copy, scale=pf(4))
+    act(B("SELDK"), B("SELB"), F.Copy, scale=pf(6))
+    ts(B("RI"), B("KI"), pf(8), None, O.mult)
+    ts(B("KI"), B("RI"), 5, 31, O.arith_shift_right, O.bitwise_and)
+    cp(B("KT"), B("KI"))
+
+    def chunk(c):
+        return 1024 * c, 1024 * c + 1024
+
+    def gather(Z, R16, c, onv):
+        lo, hi = chunk(c)
+        if onv and Z == "ZV":
+            tt(B(Z, lo, hi), IN("X", R16, 64 * c, 64 * c + 64), B("WREP", lo, hi), O.subtract)
+        elif onv:
+            cp(B(Z, lo, hi), IN("X", R16, 64 * c, 64 * c + 64))
+        else:
+            act(B(Z, lo, hi), IN("X", R16, 64 * c, 64 * c + 64), F.Copy)
+
+    def scans(Z, MX, MN, c, plo):
+        lo, hi = chunk(c)
+        h = lambda: B("P1", plo + 64 * c, plo + 64 * c + 64)
+        scan(B(MX, lo, hi), B("MKX"), B(Z, lo, hi), 0.0, O.min, O.max)
+        mm(h(), B("IDH"), B(MX, lo + 15, hi, 16), False, False)
+        scan(B(MN, lo, hi), B("MKN"), B(Z, lo, hi), 0.0, O.max, O.min)
+        mm(h(), B("IDH"), B(MN, lo + 15, hi, 16), False, c == 3)
+
+    def midstart(plo, wlo):
+        mm(B("P1", plo, plo + 256), B("ROW1"), B("CQ"), True, False)
+        if wlo < 256:
+            mm(B("P1", plo + wlo, plo + 256), B("IDN"), B("W", wlo, 256), False, False)
+
+    def distances(c, onv):
+        lo, hi = chunk(c)
+        if onv:
+            act(M("DAB", T.DAB[:, 4 * c:4 * c + 4, :], 4 * c, 4 * c + 4, 1024), B("ZV", lo, hi), F.Abs)
+        else:
+            for h in range(2):
+                b, z, q = "P6" if h == 0 else "P7", lo + 512 * h, 4 * c + 2 * h
+                mm(B(b), B("ID"), B("ZV", z, z + 512), True, False)
+                mm(B(b), B("IDN"), B("WREP", z, z + 512), False, True)
+                act(M("DAB", T.DAB[:, q:q + 2, :], q, q + 2, 512), B(b), F.Abs)
+        kb = lambda: B("P0", 64 * c, 64 * c + 64)
+        mm(kb(), B("ROWS"), B("SLOT", 0, 64), True, False)
+        for p in range(16):
+            mm(kb(), sel("SELB", p), M("DAB", T.DAB[:, 4 * c:4 * c + 4, 16 * p:16 * p + 16], 4 * c, 4 * c + 4, 64), False, p == 15)
+
+    def handon(t):
+        hb, cm = "HB%d" % t, "CM%d" % t
+        act(B(hb), IN("X", "HN%d" % t, 0, 8), F.Copy)
+        used, tl = 0, []
+        for d in range(1, 4):
+            dst = T.cores[(rank + d) % 4]
+            rid, pid, _ = topo.addr(dst)
+            mask = 0
+            for e in topo.engines(core, dst)[used:used + 2]:
+                mask += 1 << e
+            used += 2
+            tl.append(RemoteDMATransfer(dst_ids=[DstId(rid=rid, pnc=pid)], dma_engine_mask=mask, remote_sem=T.sem["arr%d" % t],
+                                        src=T[hb][:, 32 * d:32 * d + 32], dst=T[cm][:, 32 * d:32 * d + 32]))
+        add("qG", [B(cm, 32, 128)], [B(hb, 32, 128)], 1.0, lambda: g.remote_dma_fused(tl, local_sem=T.sem["out%d" % t]), 4.5, "arr%d" % t)
+
+    for t in range(3):
+        p0 = 3712 + 128 * t
+        if t:
+            handon(t - 1)
+        cp(B("VB", 0, 16), B("RTS" if t & 1 else "RTF"))
+        cp(B("V16", 0, 16), B("VB", 0, 16))
+        cp(B("RV16"), IN("RT", "V16", 0, 16))
+        ts(B("N16", 0, 8), B("DX", 0, 8), float(p0 - XD), None, O.add)
+        if t == 0:
+            cp(B("N16", 8, 16), B("FNI"))
+        else:
+            ts(B("N16", 8, 16), B("DX", 0, 8), float(p0 - 128 - XD), None, O.add)
+            cp(B("X", p0, p0 + 32), B("HB%d" % (t - 1), 0, 32))
+            cp(B("X", p0 + 32, p0 + 128), B("CM%d" % (t - 1), 32, 128))
+        act(B("W"), IN("X", "N16", 0, 16), F.Copy)
+        for s in range(16):
+            cp(B("WREP", s, 1024 * NV, 16), B("W", 0, 64 * NV))
+        for s in range(16):
+            if NV < 4:
+                act(B("WREP", 1024 * NV + s, 4096, 16), B("W", 64 * NV, 256), F.Copy)
+        L, AC = "LO%d" % t, "AC%d" % (t & 1)
+        for l in range(3):
+            go = l < 2
+            for c in range(4):
+                gather("ZV", "RV16", c, c < NV)
+            nodelists()
+            act(B("VAL", 256, 512), IN("RT", "V16", 16, 32), F.Copy)
+            cp(B("RU16"), B("VAL", 256, 512))
+            pairs()
+            act(B("MR"), IN("ST", "P16", 0, 16), F.Copy)
+            tolist("P4", 0, "SELB", "MR", 0, 256)
+            if l:
+                compare("VB", 48, "P16", "KRP", "EP")
+                firsts(272)
+                for i in range(4):
+                    act(B("AA", 16 * i, 16 * i + 16), B("P2", 272, 288), F.Copy)
+            else:
+                for i in range(4):
+                    act(B("AA", 16 * i, 16 * i + 16), B(AC), F.Copy)
+            act(B("VAL", 512, 768), IN("RT", "V16", 0, 16), F.Copy)
+            for c in range(4):
+                distances(c, c < NV)
+            midstart(0, 64 * NV)
+            for c in range(4):
+                scans("ZV", "MXV", "MNV", c, 0)
+            act(B("ML", 0, 16), B("P4", 0, 16), F.Copy)
+            if go:
+                ts(B("T2", 0, 16), B("ML", 0, 16), 0.0, None, O.is_lt)
+                tt(B("T2", 16, 32), B("T2", 0, 16), B("UM", 16, 32), O.mult)
+                tt(B("T2", 32, 48), B("T2", 16, 32), B("VB", 0, 16), O.add)
+                cp(B("P16", 16, 32), B("T2", 32, 48))
+                act(B("FRW"), IN("KT", "P16", 16, 32), F.Copy)
+                tolist("P4", 32, "SELK0", "FRW", 0, 256)
+                tolist("P4", 48, "SELDK", "FRW", 0, 256)
+            tr(M("TV", T.TV[:], 0, 32, 256), B("VAL", 512, 768))
+            for e in range(2):
+                for h in range(2):
+                    i = 2 * e + h
+                    mm(M("PR", T.PR[:, :, 16 * e:16 * e + 16], 16 * e, 16 * e + 16, 128), B("SWP", 128 * i, 128 * i + 128),
+                       M("TV", T.TV[:, :, 16 * h:16 * h + 16], 16 * h, 16 * h + 16, 128), h == 0, h == 1)
+            act(B("HR", 0, 256), B("P1", 0, 256), F.Identity, bias=MAGIC)
+            act(B("QV", 256, 512), B("P1", 0, 256), F.Sign, bias=-0.5)
+            act(B("QV", 0, 256), B("HR", 0, 256), F.Abs, bias=-MAGIC)
+            tolist("P3", 0, "SELB", "QV", 0, 512)
+            act(B("GV"), B("P3", 0, 16), F.Identity, bias=B("AX", 0, 1))
+            if go:
+                ts(B("BF1", 0, 16), B("P3", 16, 32), -1.0, None, O.is_lt)
+                tt(B("BF1", 16, 32), B("BF1", 0, 16), B("P4", 48, 64), O.mult)
+                tt(B("T1", 16, 32), B("BF1", 16, 32), B("P4", 32, 48), O.add)
+            scan(B("FK"), B("RSK"), B("P0", 0, 256), 0.0, O.max, O.min)
+            tt(B("UE"), B("P0", 0, 256), B("FK"), O.is_equal)
+            act(B("NU"), B("UE"), F.Copy, bias=1.0, scale=-1.0)
+            tt(B("UN"), B("UE"), M("PR", T.PR[:, :, 0:32], 0, 32, 256), O.mult)
+            scan(B("CN"), B("NU"), B("UN"), 0.0, O.mult, O.add)
+            cp(B("C16", 0, 16), B("CN", 15, 256, 16))
+            cp(B("CL", 0, 16), B("CN", 15, 256, 16))
+            act(B("XC"), IN("X", "C16", 0, 16), F.Copy)
+            dr = lambda: B("P0", 256, 512)
+            mm(dr(), B("ROW1"), B("CQ"), True, False)
+            mm(dr(), B("IDH"), B("W"), False, False)
+            mm(dr(), B("IDH"), B("XC"), False, True)
+            act(B("RD"), dr(), F.Identity, bias=MAGIC)
+            act(B("DR"), B("RD"), F.Identity, bias=-MAGIC)
+            compare("CL", 0, "C16", "KRC", "EC")
+            ts(B("CL", 16, 32), B("CL", 0, 16), 4095.5, None, O.is_lt)
+            tt(B("CL", 32, 48), B("CL", 0, 16), B("DX"), O.subtract)
+            tt(B("CL", 48, 64), B("CL", 16, 32), B("CL", 32, 48), O.mult)
+            firsts(256)
+            tt(B("T2", 0, 16), B("P2", 256, 272), B("CL", 48, 64), O.mult)
+            tt(B("T2", 16, 32), B("T2", 0, 16), B("DX"), O.add)
+            cp(B("C16", 16, 32), B("T2", 16, 32))
+            for c in range(4):
+                gather("ZU", "RU16", c, c >= 4 - NU)
+            midstart(256, 0)
+            for c in range(4):
+                scans("ZU", "MXU", "MNU", c, 256)
+            cp(OUT("X", "C16", 16, 32), B("DR"))
+            tt(B("ML", 16, 24), B("ML", 8, 16), B("ML", 8, 16), O.mult)
+            ts(B("ML", 24, 32), B("ML", 16, 24), float((16 * t + 24) ** 2), None, O.is_lt)
+            tt(B("AA", 8, 16), B("AA", 24, 32), B("ML", 24, 32), O.mult)
+            act(B("VB", 16, 32), B("VB", 0, 16), F.Copy)
+            tt(B("TD"), B("VB"), B("D64"), O.subtract)
+            tt(B("TD"), B("TD"), B("AA"), O.mult)
+            tt(B("VAL", 0, 128), B("VAL", 512, 640), B("HI%d" % t), O.min)
+            act(B("VAL", 128, 256), B("VAL", 640, 768), F.Copy)
+            tt(B("VAL", 256, 384), B("VAL", 256, 384), B("HI%d" % t), O.min)
+            tt(B("NMF"), B("VAL", 640, 768), B("NR%d" % t), O.is_equal)
+            act(B(L, 128, 256), B("NMF"), F.Copy, scale=4096.0)
+            act(B("MS"), B("MR"), F.Sign, scale=-1.0)
+            act(B("HR", 256, 512), B("P1", 256, 512), F.Identity, bias=MAGIC)
+            act(B("QU"), B("HR", 256, 512), F.Abs, bias=-MAGIC)
+            tolist("P3", 32, "SELB", "QU", 0, 256)
+            for i in range(4):
+                tt(B("C64", 16 * i, 16 * i + 16), B("P3", 32, 48), B("GV"), O.is_lt if i else O.is_ge)
+            tt(B("TD"), B("TD"), B("C64"), O.mult)
+            tt(B("TD"), B("TD"), B("D64"), O.add)
+            cp(B("OFF"), B("TD"))
+            tt(OUT("RT", "OFF", 0, 48), B("VAL"), B(L), O.max)
+            if go:
+                cp(B("V16", 0, 16), B("T1", 16, 32))
+                act(B("VB", 0, 16), B("T1", 16, 32), F.Copy)
+                cp(B("RV16"), IN("RT", "V16", 0, 16))
+            if t < 2 or go:
+                tt(B("EXB"), B("C64", 16, 32), B("AA", 16, 32), O.mult)
+                mm(B("P4", 64, 80), B("BLK"), B("EXB"), True, True)
+                add("qV", [B("AX", 0, 1)], [B("P4", 64, 80)], 0.06,
+                    lambda: g.vector.tensor_reduce(T.AX[:, 0:1], T.P4[:, 64:80], AxisListType.X, O.add, negate=True))
+            add("qV", [OUT("ST", "OFF", 48, 64)], [B("MS")], 0.05 + 256 * SIG * CYC, (lambda k: lambda:
+                g.vector.tensor_scalar(T.ST[:].indirect(T.OFF[:, 48:64]), T.MS[:], k, 0.0, O.mult, O.add))(t + 2.0))
+
+    dma("qY", ext(T.yx[:, 0:2048]), B("X", 0, 2048), 512)
+    dma("qY", ext(T.yx[:, 2048:4096]), B("X", 2048, 4096), 512)
+    dma("qY", ext(T.yr[:]), B("RT", 0, 1024), 512)
+    ts(B("MJ", 0, 16), B("MI", 0, 16), 1, None, O.arith_shift_right)
+    ts(B("MJ", 16, 32), B("MI", 0, 16), 1, None, O.bitwise_and)
+    cp(B("MF", 0, 32), B("MJ", 0, 32))
+    ts(B("MF", 32, 48), B("MF", 0, 16), pf(1), None, O.is_equal)
+    ts(B("MF", 16, 32), B("MF", 16, 32), pf(6), pf(4), O.mult, O.add)
+    tt(B("SELY"), B("MF", 16, 32), B("MF", 32, 48), O.mult)
+    tt(B("KH", 512, 1024), B("KT", 512, 1024), B("KT", 0, 512), O.subtract)
+    ts(B("KH", 0, 512), B("ST", 0, 512), 0.0, None, O.is_lt)
+    tt(B("KH", 0, 512), B("KH", 0, 512), B("KH", 512, 1024), O.mult)
+    tt(B("YK", 0, 512), B("KT", 0, 512), B("KH", 0, 512), O.add)
+    tt(B("YK", 512, 1024), B("KT", 512, 1024), B("KH", 0, 512), O.subtract)
+    for h in range(2):
+        b, k = "P6" if h == 0 else "P7", 512 * h
+        mm(M(b, T[b][0:16, :], 0, 512, 512), B("SELY"), B("YK", k, k + 512), True, True)
+        act(M("KL", T.KL[0:16, k:k + 512], k, k + 512, 512), M(b, T[b][0:16, :], 0, 512, 512), F.Copy)
+    dma("qY", ext(T.yk[:]), M("KL", T.KL[0:16, :], 0, 1024, 1024), 64)
+
+    cnt, know, snap, recs = {}, {q: {} for q in Q}, {}, {}
+    nd = 0
+    for i in _plan(nodes):
+        eng, call, reads, writes, cost, lat, kind = nodes[i]
+        d = {}
+
+        def put(r):
+            d[r[3]] = max(d.get(r[3], 0), r[4])
+        for (n, lo, hi) in reads:
+            for r in recs.get(n, []):
+                if (_psum(n) and r[5] != eng) or (r[2] and r[0] < hi and lo < r[1]):
+                    put(r)
+        for (n, lo, hi) in writes:
+            ps = _psum(n)
+            for r in recs.get(n, []):
+                if (ps and r[5] != eng) or (r[0] < hi and lo < r[1] and not (ps and eng == "qP")):
+                    put(r)
+        for k in sorted(d, key=lambda x: -d[x]):
+            if know[eng].get(k, 0) < d[k]:
+                Q[eng].wait_ge(T.sem[k], d[k])
+                for x, y in snap[(k, d[k])].items():
+                    know[eng][x] = max(know[eng].get(x, 0), y)
+                know[eng][k] = max(know[eng].get(k, 0), d[k])
+        inst = call()
+        who = eng
+        if kind == "c":
+            cnt[eng] = cnt.get(eng, 0) + 1
+            key, idx = eng, cnt[eng]
+            inst.then_inc(T.sem[eng], 1)
+        elif kind == "d":
+            key, idx, who = "d%d" % nd, 16, "dma"
+            nd += 1
+            inst.then_inc(T.sem[key], 16)
+        else:
+            key, idx, who = kind, 6, "remote"
+        snap[(key, idx)] = dict(know[eng])
+        for (n, lo, hi) in writes:
+            recs[n] = [r for r in recs.get(n, []) if not (lo <= r[0] and r[1] <= hi)]
+        for (n, lo, hi) in writes:
+            recs[n].append((lo, hi, True, key, idx, who))
+        for (n, lo, hi) in reads:
+            l = recs.setdefault(n, [])
+            l[:] = [r for r in l if not (not r[2] and r[3] == key and lo <= r[0] and r[1] <= hi)]
+            l.append((lo, hi, False, key, idx, who))
+    for k in range(nd):
+        g.sync.wait_ge(T.sem["d%d" % k], 16)
+    for q in QS:
+        g.sync.wait_ge(T.sem[q], cnt[q])
+    for k in ("out0", "out1", "arr0", "arr1"):
+        g.sync.wait_ge(T.sem[k], 6)

@@ -6,10 +6,11 @@ XW = 4096 + 16 + 256
 XD = 4096 + 16
 RW = 1024 + 768
 SW = 512 + 256
+TS = [0.24492, 0.46212, 0.63515, 0.76159]
 MAGIC = 12582912.0
 NV = 3
-NU = 0
-CYC, PCYC, GAM, SIG, WAKE = 0.83e-3, 0.83e-3, 1.5, 3.0, 0.08
+BC, BU, BD = -1.0, 0.0, 1.0
+CYC, PCYC, GAM, SIG, WAKE = 0.83e-3, 0.83e-3, 1.5, 3.0, 0.2
 
 
 def _s(cols, dt):
@@ -17,25 +18,25 @@ def _s(cols, dt):
 
 
 SCRATCH = {
-    "X": _s(XW, BF), "RT": _s(RW, FP), "RI": _s(1024, I32), "IDX": _s(4112, FP), "KT": _s(1024, BF), "ST": _s(SW, FP),
+    "X": _s(XW, BF), "RT": _s(RW, FP), "RI": _s(1024, I32), "IDX": _s(4112, FP), "KT": _s(2048, BF), "ST": _s(SW, FP),
     "ZV": _s(4096, BF), "ZU": _s(4096, BF), "DAB": _s([16, 256], BF), "MXV": _s(4096, BF), "MNV": _s(4096, BF),
-    "MXU": _s(4096, BF), "MNU": _s(4096, BF), "YK": _s(1024, BF), "WREP": _s(4096, BF), "W": _s(256, BF),
+    "MXU": _s(4096, BF), "MNU": _s(4096, BF), "YK": _s(512, BF), "WREP": _s(4096, BF), "W": _s(256, BF),
     "MKX": _s(1024, BF), "MKN": _s(1024, BF), "RSK": _s(256, FP), "SLOT": _s(256, BF), "THR": _s(256, BF),
-    "CQ": _s(256, BF), "HALF": _s(16, BF), "ROWS": _s(128, BF), "ROWT": _s(128, BF), "ROW1": _s(128, BF),
-    "SELB": _s(2048, BF), "SEL32": _s(2048, BF), "SELK0": _s(2048, BF), "SELDK": _s(2048, BF),
+    "CQ": _s(256, BF), "HALF": _s(32, BF), "ROWS": _s(128, BF), "ROWT": _s(128, BF), "ROW1": _s(128, BF),
+    "SELB": _s(2048, BF), "SEL32": _s(2048, BF), "SELK": _s(2048, BF),
     "ID": _s(128, BF), "IDH": _s(128, BF), "IDN": _s(128, BF), "BLK": _s(128, BF), "WD": _s(128, BF), "WO": _s(128, BF),
-    "SWP": _s(512, FP), "MFH": _s([2, 4, 32], FP), "SELY": _s(16, BF),
+    "SWP": _s(512, FP), "MFH": _s([2, 4, 32], FP), "SELY": _s(32, BF), "SH": _s(128, BF),
     "PC": _s(1, I32), "PA": _s(8, I32), "PF": _s(16, FP), "MI": _s(128, I32), "MJ": _s(128, I32), "MF": _s(512, FP),
-    "LQ": _s(128, I32), "LF": _s(128, FP), "NR0": _s(128, FP), "NR1": _s(128, FP), "NR2": _s(128, FP),
+    "LQ": _s(128, I32), "PW": _s(144, FP), "PX": _s(144, FP), "NR0": _s(128, FP), "NR1": _s(128, FP), "NR2": _s(128, FP),
     "LO0": _s(768, FP), "LO1": _s(768, FP), "LO2": _s(768, FP), "HI0": _s(128, FP), "HI1": _s(128, FP), "HI2": _s(128, FP),
-    "D64": _s(64, FP), "DX": _s(16, FP), "KI": _s(1024, I32), "KH": _s(1024, FP), "KL": _s(1024, FP),
+    "D64": _s(64, FP), "DX": _s(16, FP), "KI": _s(1024, I32), "KH": _s(512, FP), "KL": _s(1024, FP),
     "RTI": _s(16, I32), "RTF": _s(16, FP), "RTS": _s(16, FP), "FNI": _s(8, I32), "SNI": _s(8, I32), "F16": _s(8, U16), "S16": _s(8, U16),
     "NMF": _s(128, FP), "GI": _s(128, I32), "GH": _s(256, BF),
     "HN0": _s(8, U16), "HN1": _s(8, U16), "N16": _s(16, U16), "HB0": _s(128, BF), "HB1": _s(128, BF), "CM0": _s(128, BF), "CM1": _s(128, BF),
-    "VB": _s(64, FP), "V16": _s(32, U16), "P16": _s(32, U16), "T1": _s(64, FP), "T2": _s(64, FP), "UM": _s(32, FP),
+    "VB": _s(64, FP), "V16": _s(32, U16), "P16": _s(48, U16), "T1": _s(64, FP), "T2": _s(64, FP), "UM": _s(32, FP),
     "RV16": _s(256, U16), "RU16": _s(256, U16), "VAL": _s(768, FP), "TV": _s([8, 32], FP),
-    "KRP": _s(256, U16), "KRC": _s(256, U16), "EP": _s([16, 272], BF), "EC": _s([16, 272], BF), "SG": _s(256, BF),
-    "AA": _s(64, FP), "AC0": _s(16, FP), "AC1": _s(16, FP), "MR": _s(256, BF), "MS": _s(256, FP), "ML": _s(32, FP), "FRW": _s(256, BF),
+    "KRP": _s(256, U16), "KRC": _s(256, U16), "EP": _s([16, 272], BF), "EC": _s([16, 272], BF), "SG": _s(512, BF),
+    "AA": _s(64, FP), "AC0": _s(16, FP), "AC1": _s(16, FP), "MS": _s(256, FP), "ML": _s(32, FP), "FRW": _s(512, BF),
     "HR": _s(512, FP), "QV": _s(512, BF), "QU": _s(256, BF), "GV": _s(16, FP), "BF1": _s(32, FP), "TD": _s(64, FP), "C64": _s(64, FP), "OFF": _s(64, U16),
     "EXB": _s(16, BF), "AX": _s(2, FP), "FK": _s(256, FP), "UE": _s(256, FP), "UN": _s(256, FP), "NU": _s(256, FP), "CN": _s(256, FP),
     "CL": _s(64, FP), "C16": _s(32, U16), "XC": _s(256, BF), "RD": _s(256, FP), "DR": _s(256, BF),
@@ -51,7 +52,7 @@ def _psum(n):
     return SCRATCH[n][0] == "psum"
 
 
-def _plan(nodes):
+def _plan(nodes, extra):
     N = len(nodes)
     succ = [[] for _ in range(N)]
     npre = [0] * N
@@ -86,6 +87,8 @@ def _plan(nodes):
         for j, w in succ[i]:
             b = max(b, prio[j] + w)
         prio[i] = b + nodes[i][5]
+        if nodes[i][0] == "qG" and nodes[i][4] < 0.7:
+            prio[i] += 100
     ready = {}
     rt = [0.0] * N
     for i in range(N):
@@ -101,7 +104,7 @@ def _plan(nodes):
                 if best is None or s < bs:
                     best, bs = q, s
         l = ready[best]
-        k = max((i for i in l if rt[i] <= bs), key=lambda i: (prio[i], -i))
+        k = max((i for i in l if rt[i] <= bs), key=lambda i: (prio[i] + extra[i], -i))
         l.remove(k)
         order.append(k)
         free[best] = bs + nodes[k][4]
@@ -118,7 +121,7 @@ def rank_program(g, core, T, topo):
     if rank is None:
         return
     Q = {"qV": g.vector, "qS": g.scalar, "qP": g.tensor, "qG": g, "qY": g.sync}
-    nodes = []
+    nodes, extra, bonus = [], [], [0.0]
 
     def B(n, lo=0, hi=None, st=1):
         t = T[n]
@@ -129,8 +132,9 @@ def rank_program(g, core, T, topo):
     def M(n, ap, lo, hi, k):
         return (ap, [(n, lo, hi)], [], k, ISZ[SCRATCH[n][2]], "p" if _psum(n) else "s")
 
-    def IN(win, off, lo, hi):
-        return (T[win][:].indirect(T[off][:, lo:hi]), [(win, 0, 1 << 20), (off, lo, hi)], [], 16 * (hi - lo), 2, "i")
+    def IN(win, off, lo, hi, w=None):
+        t = T[win][:] if w is None else T[win][:, 0:w]
+        return (t.indirect(T[off][:, lo:hi]), [(win, 0, w or 1 << 20), (off, lo, hi)], [], 16 * (hi - lo), 2, "i")
 
     def OUT(win, off, lo, hi):
         return (T[win][:].indirect(T[off][:, lo:hi]), [(win, 0, 1 << 20)], [(off, lo, hi)], 16 * (hi - lo), 2, "i")
@@ -142,6 +146,7 @@ def rank_program(g, core, T, topo):
         reads = [x for o in ins for x in o[1]] + [x for o in outs for x in o[2]]
         writes = [x for o in outs for x in o[1]]
         nodes.append((eng, call, reads, writes, cost, cost if lat is None else lat, kind))
+        extra.append(bonus[0])
 
     def vc(out, ins, two=False):
         if any(x[5] == "i" for x in ins):
@@ -182,8 +187,17 @@ def rank_program(g, core, T, topo):
         cs = [s for s in (bias, scale) if isinstance(s, tuple)]
         pb = bias[0] if isinstance(bias, tuple) else bias
         sc = scale[0] if isinstance(scale, tuple) else scale
-        c = 0.065 + x[3] * GAM * CYC if x[5] == "i" else max(64, out[3]) * CYC
-        add("qS", [out], [x] + cs, c, lambda: g.scalar.activation(a(out), a(x), f, bias=pb, scale=sc))
+        if x[5] == "i":
+            c = 0.065 + x[3] * GAM * CYC
+        elif out[5] == "i":
+            c = 0.065 + out[3] * SIG * CYC
+        else:
+            c = max(64, out[3]) * CYC
+        if f == F.Tanh:
+            call = lambda: g.scalar.activation(a(out), a(x), f)
+        else:
+            call = lambda: g.scalar.activation(a(out), a(x), f, bias=pb, scale=sc)
+        add("qS", [out], [x] + cs, c, call)
 
     def mm(out, l, r, start, stop):
         c = max(min(64, l[3]), r[3]) * PCYC * (4 if l[4] == 4 else 1)
@@ -219,7 +233,6 @@ def rank_program(g, core, T, topo):
     iota(B("PC"), [[0, 1]], 0, 1)
     iota(B("MI"), [[1, 128]], 0, 0)
     iota(B("MF", 0, 64), [[16, 64]], 0, 0)
-    iota(B("LF"), [[1, 128]], 0, 0)
     iota(B("IDX", 0, 1024), [[1, 1024]], 0, 0)
     iota(B("IDX", 1024, 4112), [[1, 3088]], 1024, 0)
     iota(B("KI"), [[0, 1024]], 0, 0)
@@ -240,7 +253,7 @@ def rank_program(g, core, T, topo):
     act(B("IDN"), B("ID"), F.Copy, scale=-1.0)
     ts(B("BLK"), B("MF", 192, 320), pf(1), None, O.is_equal)
     act(B("WO"), B("BLK"), F.Copy, scale=65536.0)
-    ms(B("SELB"), 0.0)
+    iota(B("SELB"), [[0, 2048]], 0, 0)
     for p in range(16):
         cp(B("SELB", 129 * p, 128 * p + 128, 16), B("BLK", 0, 128, 16))
     act(B("SEL32"), B("SELB"), F.Copy, scale=1.0 / 32)
@@ -257,7 +270,8 @@ def rank_program(g, core, T, topo):
     ts(B("ROW1"), B("BLK"), 0.0, pf(7), O.mult, O.add)
     ts(B("ROWS"), B("ROW1"), 1.0 / 16, None, O.mult)
     iota(B("SLOT"), [[0, 16], [1, 16]], 0, 0)
-    ms(B("HALF"), 0.5)
+    ms(B("HALF", 0, 16), 0.5)
+    ms(B("HALF", 16, 32), 0.0)
     ms(B("CQ"), -0.25)
     ts(pf(15), pf(0), 16.0, -2.5, O.is_lt, O.mult)
     tt(pf(15), pf(15), pf(3), O.mult)
@@ -273,6 +287,7 @@ def rank_program(g, core, T, topo):
     ts(B("DX"), B("MF", 0, 16), float(XD), pf(2), O.add, O.add)
     ms(B("X", 4096, XW), 0.0)
     iota(B("ST"), [[0, SW]], 1, 0)
+    act(B("ST"), B("ST"), F.Copy, scale=TS[0])
     ms(B("MKX"), 512.0)
     ms(B("MKX", 0, 1024, 16), -512.0)
     iota(B("MKN"), [[0, 1024]], -512, 0)
@@ -292,7 +307,7 @@ def rank_program(g, core, T, topo):
 
     def compare(key, klo, k16, KR, E):
         if KR == "KRP":
-            act(B("UN"), IN("IDX", k16, 0, 16), F.Copy)
+            act(B("UN"), IN("IDX", k16, 0, 16, 1024), F.Copy)
             cp(B(KR), B("UN"))
         else:
             cp(B(KR), IN("IDX", k16, 0, 16))
@@ -305,10 +320,10 @@ def rank_program(g, core, T, topo):
             mm(B("P2", 16 * q + 16, 256), B("WO"), M(E, T[E][:, q, 16:n], 272 * q + 16, 272 * q + n, n - 16), False, False)
         mm(B("P2", 0, 256), B("WD"), M(E, T[E][:, :, 0:16], 0, 16 * 272, 256), False, True)
 
-    def firsts(lo):
-        act(B("SG"), B("P2", 0, 256), F.Sign, scale=-1.0)
-        mm(B("P2", lo, lo + 16), B("ROW1"), B("HALF"), True, False)
-        tolist("P2", lo, "SEL32", "SG", 0, 256, False)
+    def firsts(lo, n=16):
+        act(B("SG", 0, 256), B("P2", 0, 256), F.Sign, scale=-1.0)
+        mm(B("P2", lo, lo + n), B("ROW1"), B("HALF", 0, n), True, False)
+        tolist("P2", lo, "SEL32", "SG", 0, 16 * n, False)
 
     for t in (0, 1):
         cp(B("VB", 0, 16), B("RTS" if t else "RTF"))
@@ -321,8 +336,8 @@ def rank_program(g, core, T, topo):
     cp(B("F16"), B("FNI"))
     cp(B("S16"), B("SNI"))
     cp(B("NR0"), IN("IDX", "F16", 0, 8))
-    ts(B("NR1"), B("LF"), 3712.0, None, O.add)
-    ts(B("NR2"), B("LF"), 3840.0, None, O.add)
+    iota(B("NR1"), [[1, 128]], 3712, 0)
+    iota(B("NR2"), [[1, 128]], 3840, 0)
     act(B("NMF"), IN("NR0", "S16", 0, 8), F.Copy)
     cp(B("GI"), B("NMF"))
     ts(B("LQ"), B("GI"), 63, None, O.bitwise_and)
@@ -334,28 +349,19 @@ def rank_program(g, core, T, topo):
             mm(B("P4", 64, 72), sel("SELB", p), B("GH", 128 * h + p, 128 * h + 128, 16), h + p == 0, h * p == 15)
     cp(B("HN0"), B("P4", 64, 72))
     ts(B("HN1"), B("SNI"), 3712.0, None, O.add)
+    iota(B("PX"), [[0, 9], [1, 16]], 0, 0)
+    ts(B("PW"), B("PX"), pf(2), None, O.is_equal)
     for t in range(3):
-        ts(B("GI"), B("MI"), float(t), None, O.add)
-        ts(B("LQ"), B("GI"), 15, None, O.bitwise_and)
-        ts(B("LF"), B("LQ"), pf(2), None, O.is_equal)
-        ts(B("MF", 384, 512), B("MF", 64, 192), 3712.0 + 128 * t, None, O.add)
-        L = "LO%d" % t
+        L, H = "LO%d" % t, "HI%d" % t
         iota(B(L, 384, 768), [[0, 384]], 0, 0)
-        tt(B(L, 0, 128), B("LF"), B("MF", 384, 512), O.mult)
+        iota(B(H), [[1, 128]], 3712 + 128 * t, 0)
+        tt(B(L, 0, 128), B("PW", t, t + 128), B(H), O.mult)
         act(B(L, 256, 384), B(L, 0, 128), F.Copy)
-        ts(B("NMF"), B("MF", 384, 512), -5000.0, None, O.add)
-        tt(B("NMF"), B("NMF"), B("LF"), O.mult)
-        act(B("HI%d" % t), B("NMF"), F.Copy, bias=5000.0)
+        iota(B(H), [[1, 128]], 128 * t - 1288, 0)
+        tt(B(H), B(H), B("PW", t, t + 128), O.mult)
+        act(B(H), B(H), F.Copy, bias=5000.0)
     ms(B("RSK"), -1.0)
     ms(B("RSK", 0, 256, 16), 100000.0)
-    iota(B("MFH"), [[0, 2], [32, 4], [0, 32]], -1000, 0)
-    for h in range(2):
-        iota(M("MFH", T.MFH[:, h, :, 16 * h:16 * h + 16], 0, 2, 64), [[32, 4], [1, 16]], 16 * h, 0)
-    for e in range(2):
-        for h in range(2):
-            i = 2 * e + h
-            ts(B("T1", i, i + 1), pf(0), -16.0 * (e - h), None, O.add)
-            ts(B("SWP", 128 * i, 128 * i + 128), M("MFH", T.MFH[:, h, :, :], 0, 2, 128), B("T1", i, i + 1), None, O.is_equal)
     for (c, p, v) in ((4, 0, 32.0), (10, 1, 1.0), (5, 2, 32.0), (11, 3, 1.0)):
         ts(pf(c), pf(2), float(p), v, O.is_equal, O.mult)
     tt(pf(9), pf(10), pf(11), O.add)
@@ -366,21 +372,36 @@ def rank_program(g, core, T, topo):
     tt(pf(4), pf(4), pf(10), O.add)
     tt(pf(5), pf(5), pf(11), O.add)
     tt(pf(6), pf(5), pf(4), O.subtract)
-    act(B("SELK0"), B("SELB"), F.Copy, scale=pf(4))
-    act(B("SELDK"), B("SELB"), F.Copy, scale=pf(6))
+    act(B("SELK"), B("SELB"), F.Copy, scale=pf(4))
     ts(B("RI"), B("KI"), pf(8), None, O.mult)
     ts(B("KI"), B("RI"), 5, 31, O.arith_shift_right, O.bitwise_and)
-    cp(B("KT"), B("KI"))
+    cp(B("KT", 0, 1024), B("KI"))
+    ts(B("T1", 4, 5), pf(0), -2.0, None, O.add)
+    ts(pf(12), pf(4), 0.0, None, O.is_gt)
+    ts(pf(13), pf(5), 0.0, None, O.is_gt)
+    ts(B("SWP", 0, 128), B("MF", 64, 192), B("T1", 4, 5), pf(13), O.is_equal, O.mult)
+    ts(B("SWP", 128, 256), B("ID"), pf(12), None, O.mult)
+    tt(B("SH"), B("SWP", 0, 128), B("SWP", 128, 256), O.subtract)
+    for h in range(2):
+        b = "P6" if h == 0 else "P7"
+        mm(B(b), B("SH"), B("KT", 512 * h, 512 * h + 512), True, True)
+        act(B("KT", 1024 + 512 * h, 1536 + 512 * h), B(b), F.Copy)
+    iota(B("MFH"), [[0, 2], [32, 4], [0, 32]], -1000, 0)
+    for h in range(2):
+        iota(M("MFH", T.MFH[:, h, :, 16 * h:16 * h + 16], 0, 2, 64), [[32, 4], [1, 16]], 16 * h, 0)
+    for e in range(2):
+        for h in range(2):
+            i = 2 * e + h
+            ts(B("T1", i, i + 1), pf(0), -16.0 * (e - h), None, O.add)
+            ts(B("SWP", 128 * i, 128 * i + 128), M("MFH", T.MFH[:, h, :, :], 0, 2, 128), B("T1", i, i + 1), None, O.is_equal)
 
     def chunk(c):
         return 1024 * c, 1024 * c + 1024
 
     def gather(Z, R16, c, onv):
         lo, hi = chunk(c)
-        if onv and Z == "ZV":
+        if onv:
             tt(B(Z, lo, hi), IN("X", R16, 64 * c, 64 * c + 64), B("WREP", lo, hi), O.subtract)
-        elif onv:
-            cp(B(Z, lo, hi), IN("X", R16, 64 * c, 64 * c + 64))
         else:
             act(B(Z, lo, hi), IN("X", R16, 64 * c, 64 * c + 64), F.Copy)
 
@@ -456,31 +477,33 @@ def rank_program(g, core, T, topo):
             act(B("VAL", 256, 512), IN("RT", "V16", 16, 32), F.Copy)
             cp(B("RU16"), B("VAL", 256, 512))
             pairs()
-            act(B("MR"), IN("ST", "P16", 0, 16), F.Copy)
-            tolist("P4", 0, "SELB", "MR", 0, 256)
+            act(B("SG", 256, 512), IN("ST", "P16", 0, 16), F.Copy)
             if l:
                 compare("VB", 48, "P16", "KRP", "EP")
-                firsts(272)
+                firsts(272, 32)
                 for i in range(4):
                     act(B("AA", 16 * i, 16 * i + 16), B("P2", 272, 288), F.Copy)
             else:
+                tolist("P2", 288, "SEL32", "SG", 256, 512)
                 for i in range(4):
                     act(B("AA", 16 * i, 16 * i + 16), B(AC), F.Copy)
+            act(B("ML", 0, 16), B("P2", 288, 304), F.Copy)
             act(B("VAL", 512, 768), IN("RT", "V16", 0, 16), F.Copy)
+            bonus[0] = BD
             for c in range(4):
                 distances(c, c < NV)
+            bonus[0] = 0.0
             midstart(0, 64 * NV)
             for c in range(4):
                 scans("ZV", "MXV", "MNV", c, 0)
-            act(B("ML", 0, 16), B("P4", 0, 16), F.Copy)
             if go:
                 ts(B("T2", 0, 16), B("ML", 0, 16), 0.0, None, O.is_lt)
                 tt(B("T2", 16, 32), B("T2", 0, 16), B("UM", 16, 32), O.mult)
                 tt(B("T2", 32, 48), B("T2", 16, 32), B("VB", 0, 16), O.add)
                 cp(B("P16", 16, 32), B("T2", 32, 48))
-                act(B("FRW"), IN("KT", "P16", 16, 32), F.Copy)
-                tolist("P4", 32, "SELK0", "FRW", 0, 256)
-                tolist("P4", 48, "SELDK", "FRW", 0, 256)
+                ts(B("P16", 32, 48), B("T2", 32, 48), 1024.0, None, O.add)
+                act(B("FRW"), IN("KT", "P16", 16, 48), F.Copy)
+                tolist("P4", 32, "SELK", "FRW", 0, 512)
             tr(M("TV", T.TV[:], 0, 32, 256), B("VAL", 512, 768))
             for e in range(2):
                 for h in range(2):
@@ -496,6 +519,7 @@ def rank_program(g, core, T, topo):
                 ts(B("BF1", 0, 16), B("P3", 16, 32), -1.0, None, O.is_lt)
                 tt(B("BF1", 16, 32), B("BF1", 0, 16), B("P4", 48, 64), O.mult)
                 tt(B("T1", 16, 32), B("BF1", 16, 32), B("P4", 32, 48), O.add)
+            bonus[0] = BC
             scan(B("FK"), B("RSK"), B("P0", 0, 256), 0.0, O.max, O.min)
             tt(B("UE"), B("P0", 0, 256), B("FK"), O.is_equal)
             act(B("NU"), B("UE"), F.Copy, bias=1.0, scale=-1.0)
@@ -518,14 +542,17 @@ def rank_program(g, core, T, topo):
             tt(B("T2", 0, 16), B("P2", 256, 272), B("CL", 48, 64), O.mult)
             tt(B("T2", 16, 32), B("T2", 0, 16), B("DX"), O.add)
             cp(B("C16", 16, 32), B("T2", 16, 32))
+            bonus[0] = BU
             for c in range(4):
-                gather("ZU", "RU16", c, c >= 4 - NU)
+                gather("ZU", "RU16", c, False)
             midstart(256, 0)
             for c in range(4):
                 scans("ZU", "MXU", "MNU", c, 256)
+            bonus[0] = BC
             cp(OUT("X", "C16", 16, 32), B("DR"))
+            bonus[0] = 0.0
             tt(B("ML", 16, 24), B("ML", 8, 16), B("ML", 8, 16), O.mult)
-            ts(B("ML", 24, 32), B("ML", 16, 24), float((16 * t + 24) ** 2), None, O.is_lt)
+            ts(B("ML", 24, 32), B("ML", 16, 24), ((TS[t] + TS[t + 1]) / 4) ** 2, None, O.is_lt)
             tt(B("AA", 8, 16), B("AA", 24, 32), B("ML", 24, 32), O.mult)
             act(B("VB", 16, 32), B("VB", 0, 16), F.Copy)
             tt(B("TD"), B("VB"), B("D64"), O.subtract)
@@ -535,7 +562,8 @@ def rank_program(g, core, T, topo):
             tt(B("VAL", 256, 384), B("VAL", 256, 384), B("HI%d" % t), O.min)
             tt(B("NMF"), B("VAL", 640, 768), B("NR%d" % t), O.is_equal)
             act(B(L, 128, 256), B("NMF"), F.Copy, scale=4096.0)
-            act(B("MS"), B("MR"), F.Sign, scale=-1.0)
+            act(B("MS"), B("SG", 256, 512), F.Sign, scale=-1.0)
+            act(B("MS"), B("MS"), F.Copy, scale=0.25 * (t + 2))
             act(B("HR", 256, 512), B("P1", 256, 512), F.Identity, bias=MAGIC)
             act(B("QU"), B("HR", 256, 512), F.Abs, bias=-MAGIC)
             tolist("P3", 32, "SELB", "QU", 0, 256)
@@ -554,8 +582,7 @@ def rank_program(g, core, T, topo):
                 mm(B("P4", 64, 80), B("BLK"), B("EXB"), True, True)
                 add("qV", [B("AX", 0, 1)], [B("P4", 64, 80)], 0.06,
                     lambda: g.vector.tensor_reduce(T.AX[:, 0:1], T.P4[:, 64:80], AxisListType.X, O.add, negate=True))
-            add("qV", [OUT("ST", "OFF", 48, 64)], [B("MS")], 0.05 + 256 * SIG * CYC, (lambda k: lambda:
-                g.vector.tensor_scalar(T.ST[:].indirect(T.OFF[:, 48:64]), T.MS[:], k, 0.0, O.mult, O.add))(t + 2.0))
+            act(OUT("ST", "OFF", 48, 64), B("MS"), F.Tanh)
 
     dma("qY", ext(T.yx[:, 0:2048]), B("X", 0, 2048), 512)
     dma("qY", ext(T.yx[:, 2048:4096]), B("X", 2048, 4096), 512)
@@ -565,21 +592,23 @@ def rank_program(g, core, T, topo):
     cp(B("MF", 0, 32), B("MJ", 0, 32))
     ts(B("MF", 32, 48), B("MF", 0, 16), pf(1), None, O.is_equal)
     ts(B("MF", 16, 32), B("MF", 16, 32), pf(6), pf(4), O.mult, O.add)
-    tt(B("SELY"), B("MF", 16, 32), B("MF", 32, 48), O.mult)
-    tt(B("KH", 512, 1024), B("KT", 512, 1024), B("KT", 0, 512), O.subtract)
-    ts(B("KH", 0, 512), B("ST", 0, 512), 0.0, None, O.is_lt)
-    tt(B("KH", 0, 512), B("KH", 0, 512), B("KH", 512, 1024), O.mult)
-    tt(B("YK", 0, 512), B("KT", 0, 512), B("KH", 0, 512), O.add)
-    tt(B("YK", 512, 1024), B("KT", 512, 1024), B("KH", 0, 512), O.subtract)
+    tt(B("SELY", 0, 16), B("MF", 16, 32), B("MF", 32, 48), O.mult)
+    ts(B("SELY", 16, 32), B("SELY", 0, 16), -1.0, None, O.mult)
+    mm(B("P6"), B("ID"), B("KT", 512, 1024), True, False)
+    mm(B("P6"), B("IDN"), B("KT", 0, 512), False, True)
+    ts(B("KH"), B("ST", 0, 512), 0.0, None, O.is_lt)
+    tt(B("YK"), B("P6"), B("KH"), O.mult)
     for h in range(2):
-        b, k = "P6" if h == 0 else "P7", 512 * h
-        mm(M(b, T[b][0:16, :], 0, 512, 512), B("SELY"), B("YK", k, k + 512), True, True)
-        act(M("KL", T.KL[0:16, k:k + 512], k, k + 512, 512), M(b, T[b][0:16, :], 0, 512, 512), F.Copy)
+        b = "P7" if h == 0 else "P1"
+        o = lambda: M(b, T[b][0:16, :], 0, 512, 512)
+        mm(o(), B("SELY", 0, 16), B("KT", 512 * h, 512 * h + 512), True, False)
+        mm(o(), B("SELY", 16 * h, 16 * h + 16), B("YK"), False, True)
+        act(M("KL", T.KL[0:16, 512 * h:512 * h + 512], 512 * h, 512 * h + 512, 512), o(), F.Copy)
     dma("qY", ext(T.yk[:]), M("KL", T.KL[0:16, :], 0, 1024, 1024), 64)
 
     cnt, know, snap, recs = {}, {q: {} for q in Q}, {}, {}
     nd = 0
-    for i in _plan(nodes):
+    for i in _plan(nodes, extra):
         eng, call, reads, writes, cost, lat, kind = nodes[i]
         d = {}
 

from concourse.bass import DstId, RemoteDMATransfer
from concourse.mybir import AluOpType as O, ActivationFunctionType as F, AxisListType

BF, FP, I32, U16 = "bfloat16", "float32", "int32", "uint16"
XW = 4096 + 16 + 256
XD = 4096 + 16
RW = 1024 + 768
SW = 512 + 256
TS = [0.24492, 0.46212, 0.63515, 0.76159]
MAGIC = 12582912.0
NV = 3
BC, BU, BD = -1.0, 0.0, 1.0
CYC, PCYC, GAM, SIG, WAKE = 0.83e-3, 0.83e-3, 1.5, 3.0, 0.2


def _s(cols, dt):
    return ("sbuf", [128] + (cols if isinstance(cols, list) else [cols]), dt)


SCRATCH = {
    "X": _s(XW, BF), "RT": _s(RW, FP), "RI": _s(1024, I32), "IDX": _s(4112, FP), "KT": _s(2048, BF), "ST": _s(SW, FP),
    "ZV": _s(4096, BF), "ZU": _s(4096, BF), "DAB": _s([16, 256], BF), "MXV": _s(4096, BF), "MNV": _s(4096, BF),
    "MXU": _s(4096, BF), "MNU": _s(4096, BF), "YK": _s(512, BF), "WREP": _s(4096, BF), "W": _s(256, BF),
    "MKX": _s(1024, BF), "MKN": _s(1024, BF), "RSK": _s(256, FP), "SLOT": _s(256, BF), "THR": _s(256, BF),
    "CQ": _s(256, BF), "HALF": _s(32, BF), "ROWS": _s(128, BF), "ROWT": _s(128, BF), "ROW1": _s(128, BF),
    "SELB": _s(2048, BF), "SEL32": _s(2048, BF), "SELK": _s(2048, BF),
    "ID": _s(128, BF), "IDH": _s(128, BF), "IDN": _s(128, BF), "BLK": _s(128, BF), "WD": _s(128, BF), "WO": _s(128, BF),
    "SWP": _s(512, FP), "MFH": _s([2, 4, 32], FP), "SELY": _s(32, BF), "SH": _s(128, BF),
    "PC": _s(1, I32), "PA": _s(8, I32), "PF": _s(16, FP), "MI": _s(128, I32), "MJ": _s(128, I32), "MF": _s(512, FP),
    "LQ": _s(128, I32), "PW": _s(144, FP), "PX": _s(144, FP), "NR0": _s(128, FP), "NR1": _s(128, FP), "NR2": _s(128, FP),
    "LO0": _s(768, FP), "LO1": _s(768, FP), "LO2": _s(768, FP), "HI0": _s(128, FP), "HI1": _s(128, FP), "HI2": _s(128, FP),
    "D64": _s(64, FP), "DX": _s(16, FP), "KI": _s(1024, I32), "KH": _s(512, FP), "KL": _s(1024, FP),
    "RTI": _s(16, I32), "RTF": _s(16, FP), "RTS": _s(16, FP), "FNI": _s(8, I32), "SNI": _s(8, I32), "F16": _s(8, U16), "S16": _s(8, U16),
    "NMF": _s(128, FP), "GI": _s(128, I32), "GH": _s(256, BF),
    "HN0": _s(8, U16), "HN1": _s(8, U16), "N16": _s(16, U16), "HB0": _s(128, BF), "HB1": _s(128, BF), "CM0": _s(128, BF), "CM1": _s(128, BF),
    "VB": _s(64, FP), "V16": _s(32, U16), "P16": _s(48, U16), "T1": _s(64, FP), "T2": _s(64, FP), "UM": _s(32, FP),
    "RV16": _s(256, U16), "RU16": _s(256, U16), "VAL": _s(768, FP), "TV": _s([8, 32], FP),
    "KRP": _s(256, U16), "KRC": _s(256, U16), "EP": _s([16, 272], BF), "EC": _s([16, 272], BF), "SG": _s(512, BF),
    "AA": _s(64, FP), "AC0": _s(16, FP), "AC1": _s(16, FP), "MS": _s(256, FP), "ML": _s(32, FP), "FRW": _s(512, BF),
    "HR": _s(512, FP), "QV": _s(512, BF), "QU": _s(256, BF), "GV": _s(16, FP), "BF1": _s(32, FP), "TD": _s(64, FP), "C64": _s(64, FP), "OFF": _s(64, U16),
    "EXB": _s(16, BF), "AX": _s(2, FP), "FK": _s(256, FP), "UE": _s(256, FP), "UN": _s(256, FP), "NU": _s(256, FP), "CN": _s(256, FP),
    "CL": _s(64, FP), "C16": _s(32, U16), "XC": _s(256, BF), "RD": _s(256, FP), "DR": _s(256, BF),
    "P0": ("psum", [128, 512], FP), "PR": ("psum", [128, 8, 64], FP), "P1": ("psum", [128, 512], FP), "P2": ("psum", [128, 512], FP),
    "P3": ("psum", [128, 512], FP), "P4": ("psum", [128, 512], FP), "P6": ("psum", [128, 512], FP), "P7": ("psum", [128, 512], FP),
}
QS = ["qV", "qS", "qP", "qG"]
SEMAPHORES = QS + ["d%d" % i for i in range(16)] + ["arr0", "arr1", "out0", "out1"]
ISZ = {BF: 2, U16: 2, FP: 4, I32: 4}


def _psum(n):
    return SCRATCH[n][0] == "psum"


def _plan(nodes, extra):
    N = len(nodes)
    succ = [[] for _ in range(N)]
    npre = [0] * N
    recs, lastp = {}, {}
    for i, (eng, call, reads, writes, cost, lat, kind) in enumerate(nodes):
        pre = {}
        for (n, lo, hi) in reads:
            for r in recs.get(n, []):
                if (_psum(n) and r[4] != eng) or (r[2] and r[0] < hi and lo < r[1]):
                    pre[r[3]] = WAKE
        for (n, lo, hi) in writes:
            ps = _psum(n)
            if ps and eng == "qP" and n in lastp:
                pre.setdefault(lastp[n], 0.0)
            for r in recs.get(n, []):
                if (ps and r[4] != eng) or (r[0] < hi and lo < r[1] and not (ps and eng == "qP")):
                    pre[r[3]] = WAKE
            if ps and eng == "qP":
                lastp[n] = i
        for j, w in pre.items():
            succ[j].append((i, w))
        npre[i] = len(pre)
        for (n, lo, hi) in writes:
            recs[n] = [r for r in recs.get(n, []) if not (lo <= r[0] and r[1] <= hi)]
        for (n, lo, hi) in writes:
            recs[n].append((lo, hi, True, i, eng))
        for (n, lo, hi) in reads:
            recs.setdefault(n, []).append((lo, hi, False, i, eng))
    prio = [0.0] * N
    for i in range(N - 1, -1, -1):
        b = 0.0
        for j, w in succ[i]:
            b = max(b, prio[j] + w)
        prio[i] = b + nodes[i][5]
        if nodes[i][0] == "qG" and nodes[i][4] < 0.7:
            prio[i] += 100
    ready = {}
    rt = [0.0] * N
    for i in range(N):
        if npre[i] == 0:
            ready.setdefault(nodes[i][0], []).append(i)
    free = {}
    order = []
    for _ in range(N):
        best, bs = None, 0.0
        for q, l in ready.items():
            if l:
                s = max(free.get(q, 0.0), min(rt[i] for i in l))
                if best is None or s < bs:
                    best, bs = q, s
        l = ready[best]
        k = max((i for i in l if rt[i] <= bs), key=lambda i: (prio[i] + extra[i], -i))
        l.remove(k)
        order.append(k)
        free[best] = bs + nodes[k][4]
        for j, w in succ[k]:
            rt[j] = max(rt[j], bs + nodes[k][5] + w)
            npre[j] -= 1
            if npre[j] == 0:
                ready.setdefault(nodes[j][0], []).append(j)
    return order


def rank_program(g, core, T, topo):
    rank = T.rank_of(core)
    if rank is None:
        return
    Q = {"qV": g.vector, "qS": g.scalar, "qP": g.tensor, "qG": g, "qY": g.sync}
    nodes, extra, bonus = [], [], [0.0]

    def B(n, lo=0, hi=None, st=1):
        t = T[n]
        hi = SCRATCH[n][1][1] if hi is None else hi
        ap = t[:, lo:hi] if st == 1 else t[:, lo:hi:st]
        return (ap, [(n, lo, hi)], [], (hi - lo + st - 1) // st, ISZ[SCRATCH[n][2]], "p" if _psum(n) else "s")

    def M(n, ap, lo, hi, k):
        return (ap, [(n, lo, hi)], [], k, ISZ[SCRATCH[n][2]], "p" if _psum(n) else "s")

    def IN(win, off, lo, hi, w=None):
        t = T[win][:] if w is None else T[win][:, 0:w]
        return (t.indirect(T[off][:, lo:hi]), [(win, 0, w or 1 << 20), (off, lo, hi)], [], 16 * (hi - lo), 2, "i")

    def OUT(win, off, lo, hi):
        return (T[win][:].indirect(T[off][:, lo:hi]), [(win, 0, 1 << 20)], [(off, lo, hi)], 16 * (hi - lo), 2, "i")

    def a(o):
        return o[0]

    def add(eng, outs, ins, cost, call, lat=None, kind="c"):
        reads = [x for o in ins for x in o[1]] + [x for o in outs for x in o[2]]
        writes = [x for o in outs for x in o[1]]
        nodes.append((eng, call, reads, writes, cost, cost if lat is None else lat, kind))
        extra.append(bonus[0])

    def vc(out, ins, two=False):
        if any(x[5] == "i" for x in ins):
            return 0.05 + max(x[3] for x in ins) * GAM * CYC
        if out[5] == "i":
            return 0.05 + out[3] * SIG * CYC
        n = out[3]
        c = 0.5 * n if all(x[4] == 2 for x in ins + [out]) and not two else n
        if two and all(x[5] == "s" for x in ins):
            c = 2 * n
        return max(64, c) * CYC

    def tt(out, x, y, op):
        add("qV", [out], [x, y], vc(out, [x, y], True), lambda: g.vector.tensor_tensor(a(out), a(x), a(y), op))

    def ts(out, x, s1, s2, op0, op1=None):
        cs = [s for s in (s1, s2) if isinstance(s, tuple)]
        p1 = s1[0] if isinstance(s1, tuple) else s1
        p2 = s2[0] if isinstance(s2, tuple) else s2
        if op1 is None:
            add("qV", [out], [x] + cs, vc(out, [x]), lambda: g.vector.tensor_scalar(a(out), a(x), p1, None, op0))
        else:
            add("qV", [out], [x] + cs, vc(out, [x]), lambda: g.vector.tensor_scalar(a(out), a(x), p1, p2, op0, op1))

    def cp(out, x):
        add("qV", [out], [x], vc(out, [x]), lambda: g.vector.tensor_copy(a(out), a(x)))

    def ms(out, c):
        add("qV", [out], [], vc(out, []), lambda: g.vector.memset(a(out), c))

    def scan(out, d0, d1, init, op0, op1):
        add("qV", [out], [d0, d1], vc(out, [d0, d1]), lambda: g.vector.tensor_tensor_scan(a(out), a(d0), a(d1), init, op0, op1))

    def tr(out, x):
        add("qV", [out], [x], vc(out, [x]), lambda: g.vector.transpose(a(out), a(x)))

    def act(out, x, f, bias=0.0, scale=1.0):
        cs = [s for s in (bias, scale) if isinstance(s, tuple)]
        pb = bias[0] if isinstance(bias, tuple) else bias
        sc = scale[0] if isinstance(scale, tuple) else scale
        if x[5] == "i":
            c = 0.065 + x[3] * GAM * CYC
        elif out[5] == "i":
            c = 0.065 + out[3] * SIG * CYC
        else:
            c = max(64, out[3]) * CYC
        if f == F.Tanh:
            call = lambda: g.scalar.activation(a(out), a(x), f)
        else:
            call = lambda: g.scalar.activation(a(out), a(x), f, bias=pb, scale=sc)
        add("qS", [out], [x] + cs, c, call)

    def mm(out, l, r, start, stop):
        c = max(min(64, l[3]), r[3]) * PCYC * (4 if l[4] == 4 else 1)
        add("qP", [out], [l, r], c, lambda: g.tensor.matmul(a(out), a(l), a(r), start, stop))

    def iota(out, pattern, base, cm):
        add("qG", [out], [], 0.13 + 2 * out[3] * CYC,
            lambda: g.iota(a(out), pattern, base, cm, allow_small_or_imprecise_dtypes=True))

    def dma(eng, out, in_, kb):
        add(eng, [out], [in_], 0.06, lambda: Q[eng].dma_start(a(out), a(in_)), 2.0 + kb / 250.0, "d")

    def ext(ap):
        return (ap, [], [], 0, 4, "d")

    def sel(n, p):
        return B(n, 128 * p, 128 * p + 128)

    def tolist(ps, lo, S, row, rlo, rhi, start=True):
        w = (rhi - rlo) // 16
        for p in range(16):
            mm(B(ps, lo, lo + w), sel(S, p), B(row, rlo + p, rhi, 16), start and p == 0, p == 15)

    dma("qY", B("RTI"), ext(T.rt[:]), 8)
    dma("qS", B("RI"), ext(T.ring[:]), 512)
    dma("qY", B("X", 0, 1856), ext(T.x[:, 0:1856]), 464)
    dma("qS", B("X", 1856, 3712), ext(T.x[:, 1856:3712]), 464)
    dma("qY", B("X", 3840, 4096), ext(T.x[:, 3840:4096]), 64)
    dma("qS", B("X", 3712, 3840), ext(T.xl[:]), 32)
    dma("qY", B("FNI"), ext(T.fn[:]), 4)
    dma("qY", B("SNI"), ext(T.snd[:]), 4)

    iota(B("PC"), [[0, 1]], 0, 1)
    iota(B("MI"), [[1, 128]], 0, 0)
    iota(B("MF", 0, 64), [[16, 64]], 0, 0)
    iota(B("IDX", 0, 1024), [[1, 1024]], 0, 0)
    iota(B("IDX", 1024, 4112), [[1, 3088]], 1024, 0)
    iota(B("KI"), [[0, 1024]], 0, 0)
    for r in range(4):
        k = r // 2
        dma("qY", M("KI", T.KI[r:128:16, :], 0, 1024, 1024), ext(T.kid[k:16:2, :]), 64)

    pf = lambda i: B("PF", i, i + 1)
    ts(B("PA", 0, 1), B("PC"), 4, None, O.arith_shift_right)
    ts(B("PA", 1, 2), B("PC"), 15, None, O.bitwise_and)
    cp(B("PF", 0, 1), B("PC"))
    cp(B("PF", 1, 3), B("PA", 0, 2))
    ts(B("MJ"), B("MI"), 4, None, O.arith_shift_right)
    cp(B("MF", 64, 192), B("MI"))
    cp(B("MF", 192, 320), B("MJ"))
    ts(B("ID"), B("MF", 64, 192), pf(0), None, O.is_equal)
    act(B("IDH"), B("ID"), F.Copy, scale=0.5)
    act(B("IDN"), B("ID"), F.Copy, scale=-1.0)
    ts(B("BLK"), B("MF", 192, 320), pf(1), None, O.is_equal)
    act(B("WO"), B("BLK"), F.Copy, scale=65536.0)
    iota(B("SELB"), [[0, 2048]], 0, 0)
    for p in range(16):
        cp(B("SELB", 129 * p, 128 * p + 128, 16), B("BLK", 0, 128, 16))
    act(B("SEL32"), B("SELB"), F.Copy, scale=1.0 / 32)
    for i in range(4):
        ts(B("PA", 2 + i, 3 + i), B("PA", 1, 2), i, 1, O.arith_shift_right, O.bitwise_and)
    for i in range(4):
        ts(pf(10 + i), B("PA", 2 + i, 3 + i), 2.0 ** -(1 << i) - 1.0, 1.0, O.mult, O.add)
    tt(pf(14), pf(10), pf(11), O.mult)
    tt(pf(15), pf(12), pf(13), O.mult)
    tt(pf(14), pf(14), pf(15), O.mult)
    ts(pf(3), pf(14), 32768.0, None, O.mult)
    ts(B("WD"), B("BLK"), pf(3), None, O.mult)
    ts(pf(7), pf(0), 0.0, None, O.is_equal)
    ts(B("ROW1"), B("BLK"), 0.0, pf(7), O.mult, O.add)
    ts(B("ROWS"), B("ROW1"), 1.0 / 16, None, O.mult)
    iota(B("SLOT"), [[0, 16], [1, 16]], 0, 0)
    ms(B("HALF", 0, 16), 0.5)
    ms(B("HALF", 16, 32), 0.0)
    ms(B("CQ"), -0.25)
    ts(pf(15), pf(0), 16.0, -2.5, O.is_lt, O.mult)
    tt(pf(15), pf(15), pf(3), O.mult)
    ts(B("ROWT"), B("BLK"), 0.0, pf(15), O.mult, O.add)
    iota(B("FK"), [[0, 16], [1, 16]], 0, 0)
    ts(B("THR"), B("FK"), pf(2), None, O.is_equal)
    cp(B("RT", 0, 1024), B("RI"))
    cp(B("RTF"), B("RTI"))
    cp(B("RTS", 0, 8), B("RTI", 8, 16))
    cp(B("RTS", 8, 16), B("RTI", 0, 8))
    ts(B("D64", 0, 48), B("MF", 0, 48), 1024.0, pf(2), O.add, O.add)
    ts(B("D64", 48, 64), B("MF", 0, 16), 512.0, pf(2), O.add, O.add)
    ts(B("DX"), B("MF", 0, 16), float(XD), pf(2), O.add, O.add)
    ms(B("X", 4096, XW), 0.0)
    iota(B("ST"), [[0, SW]], 1, 0)
    act(B("ST"), B("ST"), F.Copy, scale=TS[0])
    ms(B("MKX"), 512.0)
    ms(B("MKX", 0, 1024, 16), -512.0)
    iota(B("MKN"), [[0, 1024]], -512, 0)
    ms(B("MKN", 0, 1024, 16), 512.0)
    ms(B("AX"), 0.0)

    def nodelists():
        ts(B("UM", 0, 16), B("VB", 0, 16), 512.0, 0.5, O.is_lt, O.subtract)
        ts(B("UM", 16, 32), B("UM", 0, 16), 1024.0, None, O.mult)
        tt(B("VB", 32, 48), B("VB", 0, 16), B("UM", 16, 32), O.add)
        cp(B("V16", 16, 32), B("VB", 32, 48))

    def pairs():
        tt(B("T1", 0, 16), B("VB", 0, 16), B("VB", 32, 48), O.add)
        ts(B("VB", 48, 64), B("T1", 0, 16), 0.5, -256.0, O.mult, O.add)
        cp(B("P16", 0, 16), B("VB", 48, 64))

    def compare(key, klo, k16, KR, E):
        if KR == "KRP":
            act(B("UN"), IN("IDX", k16, 0, 16, 1024), F.Copy)
            cp(B(KR), B("UN"))
        else:
            cp(B(KR), IN("IDX", k16, 0, 16))
        for q in range(16):
            n = 256 - 16 * q
            ts(M(E, T[E][:, q, 0:n], 272 * q, 272 * q + n, n), B(KR, 16 * q, 256), B(key, klo + q, klo + q + 1), None, O.is_equal)
        mm(B("P2", 0, 256), B("ROWT"), B("THR"), True, False)
        for q in range(15):
            n = 256 - 16 * q
            mm(B("P2", 16 * q + 16, 256), B("WO"), M(E, T[E][:, q, 16:n], 272 * q + 16, 272 * q + n, n - 16), False, False)
        mm(B("P2", 0, 256), B("WD"), M(E, T[E][:, :, 0:16], 0, 16 * 272, 256), False, True)

    def firsts(lo, n=16):
        act(B("SG", 0, 256), B("P2", 0, 256), F.Sign, scale=-1.0)
        mm(B("P2", lo, lo + n), B("ROW1"), B("HALF", 0, n), True, False)
        tolist("P2", lo, "SEL32", "SG", 0, 16 * n, False)

    for t in (0, 1):
        cp(B("VB", 0, 16), B("RTS" if t else "RTF"))
        nodelists()
        pairs()
        compare("VB", 48, "P16", "KRP", "EP")
        firsts(272)
        cp(B("AC%d" % t), B("P2", 272, 288))

    cp(B("F16"), B("FNI"))
    cp(B("S16"), B("SNI"))
    cp(B("NR0"), IN("IDX", "F16", 0, 8))
    iota(B("NR1"), [[1, 128]], 3712, 0)
    iota(B("NR2"), [[1, 128]], 3840, 0)
    act(B("NMF"), IN("NR0", "S16", 0, 8), F.Copy)
    cp(B("GI"), B("NMF"))
    ts(B("LQ"), B("GI"), 63, None, O.bitwise_and)
    ts(B("GI"), B("GI"), 6, None, O.arith_shift_right)
    ts(B("GH", 0, 128), B("GI"), 4.0, None, O.mult)
    ts(B("GH", 128, 256), B("LQ"), 1.0 / 16, None, O.mult)
    for h in range(2):
        for p in range(16):
            mm(B("P4", 64, 72), sel("SELB", p), B("GH", 128 * h + p, 128 * h + 128, 16), h + p == 0, h * p == 15)
    cp(B("HN0"), B("P4", 64, 72))
    ts(B("HN1"), B("SNI"), 3712.0, None, O.add)
    iota(B("PX"), [[0, 9], [1, 16]], 0, 0)
    ts(B("PW"), B("PX"), pf(2), None, O.is_equal)
    for t in range(3):
        L, H = "LO%d" % t, "HI%d" % t
        iota(B(L, 384, 768), [[0, 384]], 0, 0)
        iota(B(H), [[1, 128]], 3712 + 128 * t, 0)
        tt(B(L, 0, 128), B("PW", t, t + 128), B(H), O.mult)
        act(B(L, 256, 384), B(L, 0, 128), F.Copy)
        iota(B(H), [[1, 128]], 128 * t - 1288, 0)
        tt(B(H), B(H), B("PW", t, t + 128), O.mult)
        act(B(H), B(H), F.Copy, bias=5000.0)
    ms(B("RSK"), -1.0)
    ms(B("RSK", 0, 256, 16), 100000.0)
    for (c, p, v) in ((4, 0, 32.0), (10, 1, 1.0), (5, 2, 32.0), (11, 3, 1.0)):
        ts(pf(c), pf(2), float(p), v, O.is_equal, O.mult)
    tt(pf(9), pf(10), pf(11), O.add)
    tt(pf(8), pf(4), pf(5), O.add)
    ts(pf(8), pf(8), 1.0 / 32, None, O.mult)
    ts(pf(9), pf(9), 32.0, None, O.mult)
    tt(pf(8), pf(8), pf(9), O.add)
    tt(pf(4), pf(4), pf(10), O.add)
    tt(pf(5), pf(5), pf(11), O.add)
    tt(pf(6), pf(5), pf(4), O.subtract)
    act(B("SELK"), B("SELB"), F.Copy, scale=pf(4))
    ts(B("RI"), B("KI"), pf(8), None, O.mult)
    ts(B("KI"), B("RI"), 5, 31, O.arith_shift_right, O.bitwise_and)
    cp(B("KT", 0, 1024), B("KI"))
    ts(B("T1", 4, 5), pf(0), -2.0, None, O.add)
    ts(pf(12), pf(4), 0.0, None, O.is_gt)
    ts(pf(13), pf(5), 0.0, None, O.is_gt)
    ts(B("SWP", 0, 128), B("MF", 64, 192), B("T1", 4, 5), pf(13), O.is_equal, O.mult)
    ts(B("SWP", 128, 256), B("ID"), pf(12), None, O.mult)
    tt(B("SH"), B("SWP", 0, 128), B("SWP", 128, 256), O.subtract)
    for h in range(2):
        b = "P6" if h == 0 else "P7"
        mm(B(b), B("SH"), B("KT", 512 * h, 512 * h + 512), True, True)
        act(B("KT", 1024 + 512 * h, 1536 + 512 * h), B(b), F.Copy)
    iota(B("MFH"), [[0, 2], [32, 4], [0, 32]], -1000, 0)
    for h in range(2):
        iota(M("MFH", T.MFH[:, h, :, 16 * h:16 * h + 16], 0, 2, 64), [[32, 4], [1, 16]], 16 * h, 0)
    for e in range(2):
        for h in range(2):
            i = 2 * e + h
            ts(B("T1", i, i + 1), pf(0), -16.0 * (e - h), None, O.add)
            ts(B("SWP", 128 * i, 128 * i + 128), M("MFH", T.MFH[:, h, :, :], 0, 2, 128), B("T1", i, i + 1), None, O.is_equal)

    def chunk(c):
        return 1024 * c, 1024 * c + 1024

    def gather(Z, R16, c, onv):
        lo, hi = chunk(c)
        if onv:
            tt(B(Z, lo, hi), IN("X", R16, 64 * c, 64 * c + 64), B("WREP", lo, hi), O.subtract)
        else:
            act(B(Z, lo, hi), IN("X", R16, 64 * c, 64 * c + 64), F.Copy)

    def scans(Z, MX, MN, c, plo):
        lo, hi = chunk(c)
        h = lambda: B("P1", plo + 64 * c, plo + 64 * c + 64)
        scan(B(MX, lo, hi), B("MKX"), B(Z, lo, hi), 0.0, O.min, O.max)
        mm(h(), B("IDH"), B(MX, lo + 15, hi, 16), False, False)
        scan(B(MN, lo, hi), B("MKN"), B(Z, lo, hi), 0.0, O.max, O.min)
        mm(h(), B("IDH"), B(MN, lo + 15, hi, 16), False, c == 3)

    def midstart(plo, wlo):
        mm(B("P1", plo, plo + 256), B("ROW1"), B("CQ"), True, False)
        if wlo < 256:
            mm(B("P1", plo + wlo, plo + 256), B("IDN"), B("W", wlo, 256), False, False)

    def distances(c, onv):
        lo, hi = chunk(c)
        if onv:
            act(M("DAB", T.DAB[:, 4 * c:4 * c + 4, :], 4 * c, 4 * c + 4, 1024), B("ZV", lo, hi), F.Abs)
        else:
            for h in range(2):
                b, z, q = "P6" if h == 0 else "P7", lo + 512 * h, 4 * c + 2 * h
                mm(B(b), B("ID"), B("ZV", z, z + 512), True, False)
                mm(B(b), B("IDN"), B("WREP", z, z + 512), False, True)
                act(M("DAB", T.DAB[:, q:q + 2, :], q, q + 2, 512), B(b), F.Abs)
        kb = lambda: B("P0", 64 * c, 64 * c + 64)
        mm(kb(), B("ROWS"), B("SLOT", 0, 64), True, False)
        for p in range(16):
            mm(kb(), sel("SELB", p), M("DAB", T.DAB[:, 4 * c:4 * c + 4, 16 * p:16 * p + 16], 4 * c, 4 * c + 4, 64), False, p == 15)

    def handon(t):
        hb, cm = "HB%d" % t, "CM%d" % t
        act(B(hb), IN("X", "HN%d" % t, 0, 8), F.Copy)
        used, tl = 0, []
        for d in range(1, 4):
            dst = T.cores[(rank + d) % 4]
            rid, pid, _ = topo.addr(dst)
            mask = 0
            for e in topo.engines(core, dst)[used:used + 2]:
                mask += 1 << e
            used += 2
            tl.append(RemoteDMATransfer(dst_ids=[DstId(rid=rid, pnc=pid)], dma_engine_mask=mask, remote_sem=T.sem["arr%d" % t],
                                        src=T[hb][:, 32 * d:32 * d + 32], dst=T[cm][:, 32 * d:32 * d + 32]))
        add("qG", [B(cm, 32, 128)], [B(hb, 32, 128)], 1.0, lambda: g.remote_dma_fused(tl, local_sem=T.sem["out%d" % t]), 4.5, "arr%d" % t)

    for t in range(3):
        p0 = 3712 + 128 * t
        if t:
            handon(t - 1)
        cp(B("VB", 0, 16), B("RTS" if t & 1 else "RTF"))
        cp(B("V16", 0, 16), B("VB", 0, 16))
        cp(B("RV16"), IN("RT", "V16", 0, 16))
        ts(B("N16", 0, 8), B("DX", 0, 8), float(p0 - XD), None, O.add)
        if t == 0:
            cp(B("N16", 8, 16), B("FNI"))
        else:
            ts(B("N16", 8, 16), B("DX", 0, 8), float(p0 - 128 - XD), None, O.add)
            cp(B("X", p0, p0 + 32), B("HB%d" % (t - 1), 0, 32))
            cp(B("X", p0 + 32, p0 + 128), B("CM%d" % (t - 1), 32, 128))
        act(B("W"), IN("X", "N16", 0, 16), F.Copy)
        for s in range(16):
            cp(B("WREP", s, 1024 * NV, 16), B("W", 0, 64 * NV))
        for s in range(16):
            if NV < 4:
                act(B("WREP", 1024 * NV + s, 4096, 16), B("W", 64 * NV, 256), F.Copy)
        L, AC = "LO%d" % t, "AC%d" % (t & 1)
        for l in range(3):
            go = l < 2
            for c in range(4):
                gather("ZV", "RV16", c, c < NV)
            nodelists()
            act(B("VAL", 256, 512), IN("RT", "V16", 16, 32), F.Copy)
            cp(B("RU16"), B("VAL", 256, 512))
            pairs()
            act(B("SG", 256, 512), IN("ST", "P16", 0, 16), F.Copy)
            if l:
                compare("VB", 48, "P16", "KRP", "EP")
                firsts(272, 32)
                for i in range(4):
                    act(B("AA", 16 * i, 16 * i + 16), B("P2", 272, 288), F.Copy)
            else:
                tolist("P2", 288, "SEL32", "SG", 256, 512)
                for i in range(4):
                    act(B("AA", 16 * i, 16 * i + 16), B(AC), F.Copy)
            act(B("ML", 0, 16), B("P2", 288, 304), F.Copy)
            act(B("VAL", 512, 768), IN("RT", "V16", 0, 16), F.Copy)
            bonus[0] = BD
            for c in range(4):
                distances(c, c < NV)
            bonus[0] = 0.0
            midstart(0, 64 * NV)
            for c in range(4):
                scans("ZV", "MXV", "MNV", c, 0)
            if go:
                ts(B("T2", 0, 16), B("ML", 0, 16), 0.0, None, O.is_lt)
                tt(B("T2", 16, 32), B("T2", 0, 16), B("UM", 16, 32), O.mult)
                tt(B("T2", 32, 48), B("T2", 16, 32), B("VB", 0, 16), O.add)
                cp(B("P16", 16, 32), B("T2", 32, 48))
                ts(B("P16", 32, 48), B("T2", 32, 48), 1024.0, None, O.add)
                act(B("FRW"), IN("KT", "P16", 16, 48), F.Copy)
                tolist("P4", 32, "SELK", "FRW", 0, 512)
            tr(M("TV", T.TV[:], 0, 32, 256), B("VAL", 512, 768))
            for e in range(2):
                for h in range(2):
                    i = 2 * e + h
                    mm(M("PR", T.PR[:, :, 16 * e:16 * e + 16], 16 * e, 16 * e + 16, 128), B("SWP", 128 * i, 128 * i + 128),
                       M("TV", T.TV[:, :, 16 * h:16 * h + 16], 16 * h, 16 * h + 16, 128), h == 0, h == 1)
            act(B("HR", 0, 256), B("P1", 0, 256), F.Identity, bias=MAGIC)
            act(B("QV", 256, 512), B("P1", 0, 256), F.Sign, bias=-0.5)
            act(B("QV", 0, 256), B("HR", 0, 256), F.Abs, bias=-MAGIC)
            tolist("P3", 0, "SELB", "QV", 0, 512)
            act(B("GV"), B("P3", 0, 16), F.Identity, bias=B("AX", 0, 1))
            if go:
                ts(B("BF1", 0, 16), B("P3", 16, 32), -1.0, None, O.is_lt)
                tt(B("BF1", 16, 32), B("BF1", 0, 16), B("P4", 48, 64), O.mult)
                tt(B("T1", 16, 32), B("BF1", 16, 32), B("P4", 32, 48), O.add)
            bonus[0] = BC
            scan(B("FK"), B("RSK"), B("P0", 0, 256), 0.0, O.max, O.min)
            tt(B("UE"), B("P0", 0, 256), B("FK"), O.is_equal)
            act(B("NU"), B("UE"), F.Copy, bias=1.0, scale=-1.0)
            tt(B("UN"), B("UE"), M("PR", T.PR[:, :, 0:32], 0, 32, 256), O.mult)
            scan(B("CN"), B("NU"), B("UN"), 0.0, O.mult, O.add)
            cp(B("C16", 0, 16), B("CN", 15, 256, 16))
            cp(B("CL", 0, 16), B("CN", 15, 256, 16))
            act(B("XC"), IN("X", "C16", 0, 16), F.Copy)
            dr = lambda: B("P0", 256, 512)
            mm(dr(), B("ROW1"), B("CQ"), True, False)
            mm(dr(), B("IDH"), B("W"), False, False)
            mm(dr(), B("IDH"), B("XC"), False, True)
            act(B("RD"), dr(), F.Identity, bias=MAGIC)
            act(B("DR"), B("RD"), F.Identity, bias=-MAGIC)
            compare("CL", 0, "C16", "KRC", "EC")
            ts(B("CL", 16, 32), B("CL", 0, 16), 4095.5, None, O.is_lt)
            tt(B("CL", 32, 48), B("CL", 0, 16), B("DX"), O.subtract)
            tt(B("CL", 48, 64), B("CL", 16, 32), B("CL", 32, 48), O.mult)
            firsts(256)
            tt(B("T2", 0, 16), B("P2", 256, 272), B("CL", 48, 64), O.mult)
            tt(B("T2", 16, 32), B("T2", 0, 16), B("DX"), O.add)
            cp(B("C16", 16, 32), B("T2", 16, 32))
            bonus[0] = BU
            for c in range(4):
                gather("ZU", "RU16", c, False)
            midstart(256, 0)
            for c in range(4):
                scans("ZU", "MXU", "MNU", c, 256)
            bonus[0] = BC
            cp(OUT("X", "C16", 16, 32), B("DR"))
            bonus[0] = 0.0
            tt(B("ML", 16, 24), B("ML", 8, 16), B("ML", 8, 16), O.mult)
            ts(B("ML", 24, 32), B("ML", 16, 24), ((TS[t] + TS[t + 1]) / 4) ** 2, None, O.is_lt)
            tt(B("AA", 8, 16), B("AA", 24, 32), B("ML", 24, 32), O.mult)
            act(B("VB", 16, 32), B("VB", 0, 16), F.Copy)
            tt(B("TD"), B("VB"), B("D64"), O.subtract)
            tt(B("TD"), B("TD"), B("AA"), O.mult)
            tt(B("VAL", 0, 128), B("VAL", 512, 640), B("HI%d" % t), O.min)
            act(B("VAL", 128, 256), B("VAL", 640, 768), F.Copy)
            tt(B("VAL", 256, 384), B("VAL", 256, 384), B("HI%d" % t), O.min)
            tt(B("NMF"), B("VAL", 640, 768), B("NR%d" % t), O.is_equal)
            act(B(L, 128, 256), B("NMF"), F.Copy, scale=4096.0)
            act(B("MS"), B("SG", 256, 512), F.Sign, scale=-1.0)
            act(B("MS"), B("MS"), F.Copy, scale=0.25 * (t + 2))
            act(B("HR", 256, 512), B("P1", 256, 512), F.Identity, bias=MAGIC)
            act(B("QU"), B("HR", 256, 512), F.Abs, bias=-MAGIC)
            tolist("P3", 32, "SELB", "QU", 0, 256)
            for i in range(4):
                tt(B("C64", 16 * i, 16 * i + 16), B("P3", 32, 48), B("GV"), O.is_lt if i else O.is_ge)
            tt(B("TD"), B("TD"), B("C64"), O.mult)
            tt(B("TD"), B("TD"), B("D64"), O.add)
            cp(B("OFF"), B("TD"))
            tt(OUT("RT", "OFF", 0, 48), B("VAL"), B(L), O.max)
            if go:
                cp(B("V16", 0, 16), B("T1", 16, 32))
                act(B("VB", 0, 16), B("T1", 16, 32), F.Copy)
                cp(B("RV16"), IN("RT", "V16", 0, 16))
            if t < 2 or go:
                tt(B("EXB"), B("C64", 16, 32), B("AA", 16, 32), O.mult)
                mm(B("P4", 64, 80), B("BLK"), B("EXB"), True, True)
                add("qV", [B("AX", 0, 1)], [B("P4", 64, 80)], 0.06,
                    lambda: g.vector.tensor_reduce(T.AX[:, 0:1], T.P4[:, 64:80], AxisListType.X, O.add, negate=True))
            act(OUT("ST", "OFF", 48, 64), B("MS"), F.Tanh)

    dma("qY", ext(T.yx[:, 0:2048]), B("X", 0, 2048), 512)
    dma("qY", ext(T.yx[:, 2048:4096]), B("X", 2048, 4096), 512)
    dma("qY", ext(T.yr[:]), B("RT", 0, 1024), 512)
    ts(B("MJ", 0, 16), B("MI", 0, 16), 1, None, O.arith_shift_right)
    ts(B("MJ", 16, 32), B("MI", 0, 16), 1, None, O.bitwise_and)
    cp(B("MF", 0, 32), B("MJ", 0, 32))
    ts(B("MF", 32, 48), B("MF", 0, 16), pf(1), None, O.is_equal)
    ts(B("MF", 16, 32), B("MF", 16, 32), pf(6), pf(4), O.mult, O.add)
    tt(B("SELY", 0, 16), B("MF", 16, 32), B("MF", 32, 48), O.mult)
    ts(B("SELY", 16, 32), B("SELY", 0, 16), -1.0, None, O.mult)
    mm(B("P6"), B("ID"), B("KT", 512, 1024), True, False)
    mm(B("P6"), B("IDN"), B("KT", 0, 512), False, True)
    ts(B("KH"), B("ST", 0, 512), 0.0, None, O.is_lt)
    tt(B("YK"), B("P6"), B("KH"), O.mult)
    for h in range(2):
        b = "P7" if h == 0 else "P1"
        o = lambda: M(b, T[b][0:16, :], 0, 512, 512)
        mm(o(), B("SELY", 0, 16), B("KT", 512 * h, 512 * h + 512), True, False)
        mm(o(), B("SELY", 16 * h, 16 * h + 16), B("YK"), False, True)
        act(M("KL", T.KL[0:16, 512 * h:512 * h + 512], 512 * h, 512 * h + 512, 512), o(), F.Copy)
    dma("qY", ext(T.yk[:]), M("KL", T.KL[0:16, :], 0, 1024, 1024), 64)

    cnt, know, snap, recs = {}, {q: {} for q in Q}, {}, {}
    nd = 0
    for i in _plan(nodes, extra):
        eng, call, reads, writes, cost, lat, kind = nodes[i]
        d = {}

        def put(r):
            d[r[3]] = max(d.get(r[3], 0), r[4])
        for (n, lo, hi) in reads:
            for r in recs.get(n, []):
                if (_psum(n) and r[5] != eng) or (r[2] and r[0] < hi and lo < r[1]):
                    put(r)
        for (n, lo, hi) in writes:
            ps = _psum(n)
            for r in recs.get(n, []):
                if (ps and r[5] != eng) or (r[0] < hi and lo < r[1] and not (ps and eng == "qP")):
                    put(r)
        for k in sorted(d, key=lambda x: -d[x]):
            if know[eng].get(k, 0) < d[k]:
                Q[eng].wait_ge(T.sem[k], d[k])
                for x, y in snap[(k, d[k])].items():
                    know[eng][x] = max(know[eng].get(x, 0), y)
                know[eng][k] = max(know[eng].get(k, 0), d[k])
        inst = call()
        who = eng
        if kind == "c":
            cnt[eng] = cnt.get(eng, 0) + 1
            key, idx = eng, cnt[eng]
            inst.then_inc(T.sem[eng], 1)
        elif kind == "d":
            key, idx, who = "d%d" % nd, 16, "dma"
            nd += 1
            inst.then_inc(T.sem[key], 16)
        else:
            key, idx, who = kind, 6, "remote"
        snap[(key, idx)] = dict(know[eng])
        for (n, lo, hi) in writes:
            recs[n] = [r for r in recs.get(n, []) if not (lo <= r[0] and r[1] <= hi)]
        for (n, lo, hi) in writes:
            recs[n].append((lo, hi, True, key, idx, who))
        for (n, lo, hi) in reads:
            l = recs.setdefault(n, [])
            l[:] = [r for r in l if not (not r[2] and r[3] == key and lo <= r[0] and r[1] <= hi)]
            l.append((lo, hi, False, key, idx, who))
    for k in range(nd):
        g.sync.wait_ge(T.sem["d%d" % k], 16)
    for q in QS:
        g.sync.wait_ge(T.sem[q], cnt[q])
    for k in ("out0", "out1", "arr0", "arr1"):
        g.sync.wait_ge(T.sem[k], 6)
